import numpy as np, ml_dtypes
CORES = [16,17,18,19,32,33,34,35]
N = 8
BF = ml_dtypes.bfloat16
W, C, TS, HOP, SA, SX = 4096, 192, 5, 3, 3, 5
def rise(rng):
    return np.sort(rng.integers(0, W - 15, (N, 8, 16, C)), axis=2) + np.arange(16)[:, None]
def inner(rng):
    m = np.sort(rng.integers(0, W - 15, (N, 8, 14, C)), axis=2) + np.arange(14)[:, None] + 1
    return np.concatenate([np.zeros((N, 8, 1, C), np.int64), m, np.full((N, 8, 1, C), W - 1)], axis=2)
def split(rng):
    k = np.arange(16)[:, None]
    return np.where(k < rng.integers(0, 17, (N, 8, 1, C)), k, W - 16 + k)
def signs(rng):
    return 2 * rng.integers(0, 2, (N, 8, C)) - 1
def pack(x, r, a, s, w):
    return {"xt": np.ascontiguousarray(x).reshape(N, 128, W).astype(np.float32).astype(BF), "rl": np.ascontiguousarray(r).reshape(N, 128, C).astype(np.int32),
            "av": np.ascontiguousarray(a).reshape(N, 128, C).astype(np.float32).astype(BF), "sg": s.astype(np.int32), "wt": np.ascontiguousarray(w).reshape(N, 128, 1).astype(np.int32)}
def setup_inputs(rng):
    return pack(rng.integers(0, 256, (N, 8, 16, W)), rise(rng), rng.integers(0, 256, (N, 8, 16, C)), signs(rng), rng.integers(1, 256, (N, 8, 16)))
def setup_inputs_corners(rng):
    k = np.arange(16)[:, None]; z = int(rng.integers(0, N)); z1 = (z + HOP) % N
    x = rng.integers(0, 256, (N, 8, 16, W)); kind = rng.integers(0, 16, (N, 8, 1, W)); x = np.where(kind == 0, 0, np.where(kind == 1, 255, x)); x[np.arange(N) != z1, ..., ::64] = 0
    zero = 64 * (np.sort(rng.integers(0, W // 64 - 15, (N, 8, 16, C)), axis=2) + k)
    high = 64 * (2 * np.sort(rng.integers(0, W // 128 - 7, (N, 8, 16, C)), axis=2) + k) + 32
    typ = rng.integers(0, 8, (N, 8, 1, C)); typ[..., 8:16] = np.arange(8); typ[:, 2, :, C // 2:C - 1] = 8; typ[..., 5] = 7; typ[..., C - 1] = 7; typ[z] = 7
    r = np.choose(typ, [k, W - 16 + k, rng.integers(0, W - 15, (N, 8, 1, C)) + k, inner(rng), split(rng), rng.integers(0, W - 30, (N, 8, 1, C)) + 2 * k, rise(rng), zero, high])
    ka = rng.integers(0, 5, (N, 8, 1, C)); a = np.where(ka == 0, 0, np.where(ka == 1, 255, rng.integers(0, 256, (N, 8, 16, C))))
    a[z, :, :, 0] = rng.integers(1, 256, (8, 16))
    kw = rng.integers(0, 4, (N, 8, 1)); w = np.where(kw == 0, 1, np.where(kw == 1, 255, rng.integers(1, 256, (N, 8, 16))))
    w[:, 2, 0] = 1; w[:, 2, 1] = 16
    y = x[:, 2, :, 32::64]
    rem = (np.where(np.arange(W // 64) % 2 == 0, 4089, 4087) - np.sum(w[:, 2, 2:, None] * y[:, 2:], axis=1)) & 4095
    y[:, 0] = rem & 15; y[:, 1] = rem >> 4
    return pack(x, r, a, signs(rng), w)
def setup_inputs_ends(rng):
    k = np.arange(16)[:, None]; S = W >> 4
    w = 1 + 254 * rng.integers(0, 2, (N, 8, 16)); w[..., 0] = 1; w[..., 15] = 1; w[..., 7] = 255; w[:, 3] = 255; w[:, 5] = 1
    top = np.zeros((16, 1), np.int64); top[[0, 7, 15]] = 1
    kind = rng.integers(0, 6, (N, 8, 1, W)); x = rng.integers(0, 2, (N, 8, 16, W))
    x = np.where(kind == 0, 0, np.where(kind == 1, 1, np.where(kind == 2, top, x)))
    x[..., ::S] = top
    m = rng.random((N, 8, 16)) < 0.4; m[:, ::2] = False; m[..., 15] = True; m[:, 7, rng.integers(0, 4)] = True
    x[..., S - 1::S] = np.where(m[:, :, None, :], 1, x[..., S - 1::S]); x[:, :, 3, S - 1::S] = m
    ka = rng.integers(0, 4, (N, 8, 1, C)); ka[..., [0, 2, C - 2, C - 1]] = 0; ka[..., [1, C - 3]] = 1
    a = np.where(ka == 0, 0, np.where(ka == 1, 1, rng.integers(0, 2, (N, 8, 16, C))))
    typ = np.array([0, 0, 0, 0, 0, 0, 0, 1, 1, 2])[rng.integers(0, 10, (N, 8, 1, C))]; typ[..., [0, 1, 2, C - 3, C - 2, C - 1]] = 2
    return pack(255 * x, np.choose(typ, [split(rng), inner(rng), k * S]), 255 * a, signs(rng), w)
def setup_inputs_shared(rng):
    r = rise(rng); r = np.take_along_axis(r, rng.integers(0, 4, (N, 8, 1, C)), 3)
    x = rng.integers(0, 256, (N, 8, 16, W)); a = rng.integers(0, 256, (N, 8, 16, C)); s = signs(rng)
    r[:, 6] = r[:, 6, :, :1].copy(); s[:, 6] = s[:, 6, :1].copy()
    b = rng.integers(112, 144, (N, 16, 1)); far = rng.integers(0, 64, (N, 16, W)) + 192 * rng.integers(0, 2, (N, 16, W))
    for q in range(N): far[q][:, r[q, 6, :, 0]] = b[q] + rng.integers(-2, 3, (16, 16))
    x[:, 6] = far; a[:, 6] = b + rng.integers(-2, 3, (N, 16, C))
    return pack(x, r, a, s, rng.integers(1, 256, (N, 8, 16)))
def setup_inputs_spread(rng):
    x = np.minimum(np.exp2(9 * rng.random((N, 8, 1, W))) * rng.random((N, 8, 16, W)), 255).astype(np.int64)
    a = np.minimum(np.exp2(9 * rng.random((N, 8, 1, C))) * rng.random((N, 8, 16, C)), 255).astype(np.int64)
    r = np.sort((rng.random((N, 8, 16, C)) ** 3 * (W - 15)).astype(np.int64), axis=2) + np.arange(16)[:, None]
    return pack(x, r, a, signs(rng), np.clip(np.exp2(8 * rng.random((N, 8, 16))).astype(np.int64), 1, 255))
def setup_inputs_ties(rng):
    x = 100 + rng.integers(0, 3, (N, 8, 16, W)); a = 100 + rng.integers(0, 3, (N, 8, 16, C)) + rng.integers(-1, 2, (N, 8, 1, C))
    x[:, 6:] = 100 + SX * rng.integers(-1, 2, (N, 2, 16, W)); a[:, 6:] = 100 + SA * rng.integers(-1, 2, (N, 2, 16, C))
    return pack(x, rise(rng), a, signs(rng), rng.integers(1, 256, (N, 8, 16)))
def check_inputs(d):
    bad = []
    for k, lo, hi in (("xt", 0, 255), ("rl", 0, W - 1), ("av", 0, 255), ("sg", -1, 1), ("wt", 1, 255)):
        v = np.asarray(d[k]).astype(np.float64)
        if not np.all((v >= lo) & (v <= hi)): bad.append("range of " + k)
        elif not np.all(v == np.floor(v)): bad.append("whole numbers of " + k)
    if np.any(np.asarray(d["sg"]) == 0): bad.append("signs of sg")
    r = np.asarray(d["rl"]).astype(np.int64).reshape(N, 8, 16, C)
    if not np.all(r[:, :, 1:] > r[:, :, :-1]): bad.append("rl not rising")
    return bad
def pick(x, ix):
    return np.take_along_axis(x, ix.reshape(8, 1, 16 * C), 2).reshape(8, 16, 16, C)
def reference(xt, rl, av, sg, wt):
    x = xt.astype(np.float32).astype(np.int64).reshape(N, 8, 16, W); R = rl.astype(np.int64).reshape(N, 8, 16, C)
    A = av.astype(np.float32).astype(np.int64).reshape(N, 8, 16, C); sig = sg.astype(np.int64).reshape(N, 8, C)
    w = wt.astype(np.int64).reshape(N, 8, 16, 1, 1); cnt = np.zeros((N, C), np.int64); kk = np.arange(16)[None, :, None]
    for t in range(TS):
        for r in range(N):
            p = (r + HOP * t) % N; X = x[p]; L = R[r].copy(); a = A[r].copy(); s0 = sig[r].copy()
            u = np.sum(w[p] * pick(X, L), axis=1) & 4095
            h = ((u * np.roll(u, -1, axis=1) >> 5) + u + cnt[r]) & 255
            st = (np.concatenate([L[:, 1:], L[:, :1] + W], axis=1) - L) * h >> 8
            q = (L + st) & (W - 1)
            Xq = pick(X, q); E = np.where(st == 0, -1, np.sum(np.abs(Xq - a[:, :, None, :]), axis=1))
            k = np.argmax(E, axis=1); e = np.max(E, axis=1)
            qb = np.take_along_axis(q, k[:, None, :], 1)[:, 0]; xq = np.take_along_axis(Xq, k[:, None, None, :], 2)[:, :, 0]
            s = np.where(np.sum(xq > a, axis=1) >= 8, 1, -1)
            out = k == 15; first = out & (qb < L[:, 0])
            shift = out & (s != np.where(first, s0, -s0))
            place = np.where(out, np.where(first != shift, 0, 15), k + (s != s0 * (1 - 2 * (k & 1))))
            col = np.take_along_axis(L, place[:, None, :], 1)[:, 0]; xl = np.take_along_axis(X, col[:, None, :], 2)
            go = e > np.sum(np.abs(xl - a), axis=1)
            qn = qb[:, None, :]; new = np.where(kk == place[:, None, :], qn, L)
            new = np.where((shift & first)[:, None, :], np.concatenate([qn, L[:, :15]], axis=1), new)
            new = np.where((shift & ~first)[:, None, :], np.concatenate([L[:, 1:], qn], axis=1), new)
            R[r] = np.where(go[:, None, :], new, L); sig[r] = np.where(go & shift, -s0, s0); cnt[r] = np.sum(go, axis=0)
            A[r] = np.where(go[:, None, :], a + np.clip(xq - a, -SA, SA), a)
            back = xl + np.clip(a - xl, -SX, SX)
            for g in range(8):
                c = np.nonzero(go[g])[0]; cols, i = np.unique(col[g, c], return_index=True)
                x[p, g][:, cols] = back[g][:, c[i]]
    return {"yr": R.reshape(N, 128, C).astype(np.float32), "ya": A.reshape(N, 128, C).astype(np.float32).astype(BF),
            "ys": sig.astype(np.float32), "yx": x.reshape(N, 128, W).astype(np.float32).astype(BF)}

@@ -1,0 +1,442 @@
+from concourse.bass import DstId, RemoteDMATransfer
+from concourse.mybir import dt, AluOpType, AxisListType, ActivationFunctionType
+
+ALU = AluOpType
+ACT = ActivationFunctionType
+W, C, TS, HOP = 4096, 192, 5, 3
+CD = C // 16
+PAD = 32
+BIG = 16777216.0
+
+SCRATCH = {
+    "X": ("sbuf", [128, W + PAD], "bfloat16"), "IOT": ("sbuf", [128, W + PAD], "float32"),
+    "G": ("sbuf", [128, 16 * C], "bfloat16"), "D": ("sbuf", [128, 16 * C], "bfloat16"),
+    "DA": ("sbuf", [128, 16 * C], "bfloat16"), "Ab": ("sbuf", [128, CD, 256], "bfloat16"),
+    "ti": ("sbuf", [128, 8], "int32"), "pf": ("sbuf", [128, 8], "float32"), "pc": ("sbuf", [128, 8], "float32"),
+    "wi": ("sbuf", [128, 1], "int32"), "wf": ("sbuf", [128, 1], "float32"),
+    "cp": ("sbuf", [128, 128], "float32"), "colm": ("sbuf", [128, C], "float32"), "colf": ("sbuf", [128, 144], "float32"),
+    "chi": ("sbuf", [128, 128], "float32"),
+    "negI": ("sbuf", [128, 128], "float32"), "vI": ("sbuf", [128, 128], "bfloat16"), "SH": ("sbuf", [128, 128], "float32"),
+    "pm1": ("sbuf", [128, 128], "float32"), "ps": ("sbuf", [128, 4], "float32"),
+    "k1": ("sbuf", [128, 152], "float32"), "k2": ("sbuf", [128, C], "float32"),
+    "diag": ("sbuf", [128, C], "bfloat16"), "m8": ("sbuf", [128, C], "float32"), "rsn": ("sbuf", [128, C], "float32"),
+    "rs1": ("sbuf", [128, C], "float32"), "BW": ("sbuf", [128, 144], "bfloat16"), "BE": ("sbuf", [128, 144], "bfloat16"),
+    "E8T": ("sbuf", [128, 128], "bfloat16"), "E8": ("sbuf", [128, 8], "bfloat16"), "zer": ("sbuf", [128, C], "bfloat16"),
+    "w01": ("sbuf", [128, 16], "bfloat16"),
+    "ob": ("sbuf", [128, CD], "uint16"), "opa": ("sbuf", [128, CD], "uint16"), "opb": ("sbuf", [128, CD], "uint16"),
+    "onx": ("sbuf", [128, CD], "uint16"),
+    "rli": ("sbuf", [128, C], "int32"), "sgi": ("sbuf", [128, C], "int32"), "sgb": ("sbuf", [128, C], "bfloat16"),
+    "r1": ("sbuf", [128, C], "float32"), "r2": ("sbuf", [128, C], "float32"), "r3": ("sbuf", [128, C], "float32"),
+    "r4": ("sbuf", [128, C], "float32"),
+    "Z": ("sbuf", [128, CD, 32], "float32"), "Zt": ("sbuf", [128, CD, 32], "float32"),
+    "sa": ("sbuf", [128, CD, 16], "float32"), "sb": ("sbuf", [128, CD, 16], "float32"),
+    "sf": ("sbuf", [128, 16], "float32"), "sx": ("sbuf", [128, C], "bfloat16"), "so": ("sbuf", [128, C], "float32"),
+    "Rf": ("sbuf", [128, C + CD], "float32"), "MF": ("sbuf", [128, C + 2 * CD], "float32"), "Rn": ("sbuf", [128, C], "float32"),
+    "gob": ("sbuf", [128, C], "bfloat16"), "nb": ("sbuf", [128, C], "float32"),
+    "i1": ("sbuf", [128, C], "int32"), "i2": ("sbuf", [128, C], "int32"), "i3": ("sbuf", [128, C], "int32"),
+    "i4": ("sbuf", [128, C], "int32"), "u": ("sbuf", [128, CD, 17], "int32"), "dh": ("sbuf", [128, C], "float32"),
+    "qi": ("sbuf", [128, C], "int32"), "qu": ("sbuf", [128, C], "uint16"), "vo": ("sbuf", [128, C], "bfloat16"),
+    "DY": ("sbuf", [128, 3 * C], "float32"), "wy": ("sbuf", [128, 3 * C], "float32"), "Yl": ("sbuf", [128, 3 * CD], "float32"),
+    "Yb": ("sbuf", [128, 3 * CD], "float32"), "o3": ("sbuf", [128, 3 * CD], "uint16"), "run": ("sbuf", [128, C], "float32"),
+    "nn": ("sbuf", [128, C], "float32"), "Kx": ("sbuf", [128, 3 * CD], "float32"), "D3": ("sbuf", [128, 3 * C], "bfloat16"),
+    "T3": ("sbuf", [128, 3 * C], "bfloat16"), "F": ("sbuf", [128, 3 * CD], "float32"), "gg": ("sbuf", [128, 2 * CD], "float32"),
+    "dl": ("sbuf", [128, 2 * CD], "float32"), "dg": ("sbuf", [128, 2 * CD], "float32"), "ee": ("sbuf", [128, 2 * CD], "float32"),
+    "te": ("sbuf", [128, 2 * CD], "float32"), "oc": ("sbuf", [128, CD], "uint16"),
+    "mm": ("sbuf", [128, C], "float32"), "rr": ("sbuf", [128, C], "float32"), "c3": ("sbuf", [128, C], "bfloat16"),
+    "ta": ("sbuf", [128, C], "bfloat16"), "Nm": ("sbuf", [128, C], "float32"), "ne": ("sbuf", [128, C], "float32"),
+    "nd": ("sbuf", [128, C], "float32"), "kn": ("sbuf", [128, CD], "float32"), "lo": ("sbuf", [128, 2 * CD], "uint16"),
+    "xl": ("sbuf", [128, C], "bfloat16"), "dx": ("sbuf", [128, C], "bfloat16"), "c5": ("sbuf", [128, C], "bfloat16"),
+    "c4": ("sbuf", [128, C], "bfloat16"),
+    "pW": ("psum", [128, 512], "float32"), "pK": ("psum", [128, 512], "float32"), "p3": ("psum", [128, 512], "float32"),
+    "pN": ("psum", [128, 512], "float32"), "pD": ("psum", [128, 512], "float32"), "pA": ("psum", [128, 512], "float32"),
+    "pB": ("psum", [128, 512], "float32"),
+}
+for _t in range(TS + 1):
+    SCRATCH["mi%d" % _t] = ("sbuf", [128, C + CD], "uint16")
+    SCRATCH["ai%d" % _t] = ("sbuf", [128, C], "bfloat16")
+for _t in range(TS):
+    SCRATCH["mo%d" % _t] = ("sbuf", [128, C + 2 * CD], "uint16")
+    SCRATCH["ao%d" % _t] = ("sbuf", [128, C], "bfloat16")
+
+SEMAPHORES = (["cV", "cS", "cP", "cG", "sent", "lx", "lr", "la", "ls", "lw", "ox", "oa", "orr", "osg"]
+              + ["rm%d" % t for t in range(1, TS + 1)] + ["ra%d" % t for t in range(1, TS + 1)])
+PSUM = ("pW", "pK", "p3", "pN", "pD", "pA", "pB")
+
+HALF = 255.0 / 512
+R_V = [(0, 2), (4, 6), (8, 9)]
+R_S = [(2, 4), (6, 8), (9, 12)]
+FILL = 1
+LATER = 0
+Q_CH = [(0, 2), (2, 4), (4, 6), (6, 8), (8, 10), (10, 11), (11, 12)]
+PE_CH = [(0, 4), (4, 8), (8, 12)]
+AB_CH = [(0, 6), (6, 12)]
+
+
+def rank_program(g, core, T, topo):
+    rank = T.rank_of(core)
+    if rank is None:
+        return
+    N = len(T.cores)
+    Q = {"V": g.vector, "S": g.scalar, "P": g.tensor, "G": g, "Y": g.sync}
+    count = {"V": 0, "S": 0, "P": 0, "G": 0}
+    known = {}
+    writer = {}
+    readers = {}
+    final = {}
+
+    def wait(e, sem, val):
+        if known.get((e, sem), 0) < val:
+            known[(e, sem)] = val
+            Q[e].wait_ge(T.sem[sem], val)
+
+    def order(e, reads, writes):
+        need = {}
+        for k in reads:
+            if k in writer:
+                s, v, we = writer[k]
+                if not (e == "P" and we == "P"):
+                    need[s] = max(need.get(s, 0), v)
+        for k in list(writes) + [k for k in reads if k in PSUM]:
+            if k in writer and not (e == "P" and writer[k][2] == "P"):
+                s, v, we = writer[k]
+                need[s] = max(need.get(s, 0), v)
+            for oe, (s, v) in readers.get(k, {}).items():
+                if oe != e or k in writes:
+                    need[s] = max(need.get(s, 0), v)
+        for s, v in need.items():
+            wait(e, s, v)
+
+    def note(e, sem, val, reads, writes):
+        for k in writes:
+            writer[k] = (sem, val, e)
+            readers[k] = {}
+        for k in reads:
+            if k not in writes:
+                readers.setdefault(k, {})[e] = (sem, val)
+        final[sem] = val
+
+    def op(e, reads, writes, call):
+        order(e, reads, writes)
+        count[e] += 1
+        call().then_inc(T.sem["c" + e], 1)
+        note(e, "c" + e, count[e], reads, writes)
+
+    def dma(e, sem, reads, writes, out, in_, slow=False):
+        order(e, reads, writes)
+        if slow:
+            Q[e].dma_start(out, in_, allow_slow_non_contiguous=True).then_inc(T.sem[sem], 16)
+        else:
+            Q[e].dma_start(out, in_).then_inc(T.sem[sem], 16)
+        note("dma" + sem, sem, final.get(sem, 0) + 16, reads, writes)
+
+    def lanes(src, dst):
+        m = 0
+        es = topo.engines(src, dst)[:8]
+        for x in es:
+            m |= 1 << x
+        return m, len(es)
+
+    def send(name, dst_name, sem, dst):
+        order("G", [name], [])
+        rid, pid, _ = topo.addr(dst)
+        m, n = lanes(core, dst)
+        g.remote_dma(T[dst_name][:], T[name][:, 0:T[dst_name].shape[1]], T.sem[sem], T.sem.sent, pid, rid, m)
+        final["sent"] = final.get("sent", 0) + n
+
+    def expect(name, sem, src):
+        n = lanes(src, core)[1]
+        writer[name] = (sem, n, "far")
+        final[sem] = n
+
+    def tt(r, w, out, a, b, o):
+        op("V", r, w, lambda: g.vector.tensor_tensor(out, a, b, o))
+
+    def ts(r, w, out, a, s1, o1, s2=None, o2=None):
+        if o2 is None:
+            op("V", r, w, lambda: g.vector.tensor_scalar(out, a, s1, None, o1))
+        else:
+            op("V", r, w, lambda: g.vector.tensor_scalar(out, a, s1, s2, o1, o2))
+
+    def cpv(r, w, out, a):
+        op("V", r, w, lambda: g.vector.tensor_copy(out, a))
+
+    def cps(r, w, out, a):
+        op("S", r, w, lambda: g.scalar.activation(out, a, ACT.Copy))
+
+    def act(r, w, out, a, func, bias, scale):
+        op("S", r, w, lambda: g.scalar.activation(out, a, func, bias=bias, scale=scale))
+
+    def mset(w, out, val):
+        op("V", [], w, lambda: g.vector.memset(out, val))
+
+    def scan(r, w, out, d0, d1, o0, o1):
+        op("V", r, w, lambda: g.vector.tensor_tensor_scan(out, d0, d1, 0.0, o0, o1))
+
+    def mm(r, w, out, lhsT, rhs, start, stop):
+        op("P", r, w, lambda: g.tensor.matmul(out, lhsT, rhs, start, stop))
+
+    def iota(w, out, pattern, base, mult):
+        op("G", [], w, lambda: g.iota(out, pattern, base, mult, allow_small_or_imprecise_dtypes=True))
+
+    def blocks(name, a, b):
+        return [(name, i) for i in range(a, b)]
+
+    def turn(src, src_keys, dst, dst_key):
+        ts(src_keys + ["pc"], ["Z0"], T.Z[:, :, 0:16], src, T.pc[:, 4:5], ALU.mult)
+        ts(src_keys + ["pf"], ["Z1"], T.Z[:, :, 16:32], src, T.pf[:, 3:4], ALU.mult)
+        op("V", ["Z0", "Z1"], ["Zt"], lambda: g.vector.transpose(T.Zt[:], T.Z[:]))
+        tt(["Zt"], [dst_key], dst, T.Zt[:, :, 0:16], T.Zt[:, :, 16:32], ALU.add)
+
+    XT = T.X[:, PAD:PAD + W]
+
+    dma("S", "lr", [], ["rli"], T.rli[:], T.rl[:])
+    dma("Y", "ls", [], ["sgi"], T.sgi[0:8, :], T.sg[:])
+    dma("Y", "lx", [], ["X"], XT, T.xt[:])
+    dma("Y", "la", [], ["ai0"], T.ai0[:], T.av[:])
+    op("G", [], ["ti0"], lambda: g.iota(T.ti[:, 0:1], [[0, 1]], 0, 1))
+    iota(["colf"], T.colf[:], [[1, 144]], 0, 0)
+    iota(["cp"], T.cp[:], [[1, 128]], 0, -1)
+    iota(["chi"], T.chi[0:8, :], [[1, 8], [0, 16]], 0, -1)
+    dma("G", "lw", [], ["wi"], T.wi[:], T.wt[:], slow=True)
+    iota(["colm"], T.colm[:], [[0, CD], [1, 16]], 0, 0)
+    iota(["DY"], T.DY[:], [[0, 3 * C]], 0, 0)
+    iota(["Kx2"], T.Kx[:, 2 * CD:3 * CD], [[0, CD]], 17 * 2048, 0)
+    iota(["w01"], T.w01[:], [[1, 16]], 0, 0)
+    iota(["sf"], T.sf[:], [[0, 16]], 0, 0)
+    iota(["IOT"], T.IOT[:], [[1, W + PAD]], 0, 0)
+
+    mset(["Xpad"], T.X[:, 0:PAD], 0.0)
+    mset(["zer"], T.zer[:], 0.0)
+    ts(["ti0"], ["ti1"], T.ti[:, 1:2], T.ti[:, 0:1], 15, ALU.bitwise_and)
+    ts(["ti0"], ["ti2"], T.ti[:, 2:3], T.ti[:, 0:1], 4, ALU.logical_shift_right)
+    ts(["ti0"], ["ti3"], T.ti[:, 3:4], T.ti[:, 0:1], 4, ALU.logical_shift_right, 1, ALU.bitwise_and)
+    ts(["ti0"], ["ti4"], T.ti[:, 4:5], T.ti[:, 0:1], 1, ALU.bitwise_and)
+    cpv(["ti0", "ti1", "ti2", "ti3", "ti4"], ["pf"], T.pf[:, 0:5], T.ti[:, 0:5])
+    ts(["pf"], ["pc1"], T.pc[:, 1:2], T.pf[:, 1:2], 0.0, ALU.is_equal, 16.0, ALU.mult)
+    ts(["cp"], ["negI"], T.negI[:], T.cp[:], 0.0, ALU.is_equal, -1.0, ALU.mult)
+    ts(["pf", "pc1"], ["pc5"], T.pc[:, 5:6], T.pf[:, 0:1], T.pc[:, 1:2], ALU.add, -1.0, ALU.add)
+    ts(["chi"], ["E8T"], T.E8T[0:8, :], T.chi[0:8, :], 0.0, ALU.is_equal)
+    ts(["colf", "pc5"], ["pm1"], T.pm1[:], T.colf[:, 0:128], T.pc[:, 5:6], ALU.is_equal)
+    act(["pf"], ["pc0"], T.pc[:, 0:1], T.pf[:, 2:3], ACT.Identity, 15.0, 16.0)
+    act(["pf"], ["pc2"], T.pc[:, 2:3], T.pf[:, 1:2], ACT.Identity, 1.0, 1.0)
+    act(["pf"], ["pc3"], T.pc[:, 3:4], T.pf[:, 4:5], ACT.Identity, 0.0, float(CD))
+    act(["pf"], ["pc4"], T.pc[:, 4:5], T.pf[:, 3:4], ACT.Identity, 1.0, -1.0)
+    act(["pf"], ["ps0"], T.ps[:, 0:1], T.pf[:, 1:2], ACT.Identity, 0.0, -1.0)
+    act(["pf"], ["ps1"], T.ps[:, 1:2], T.pf[:, 1:2], ACT.Identity, 8192.0, -8192.0)
+    act(["pf"], ["ps2"], T.ps[:, 2:3], T.pf[:, 2:3], ACT.Identity, -15.0, -16.0)
+    act(["pf"], ["ps3"], T.ps[:, 3:4], T.pf[:, 2:3], ACT.Identity, 0.0, -1.0)
+    ts(["sgi"], ["sgb"], T.sgb[0:8, :], T.sgi[0:8, :], 0.0, ALU.is_lt)
+    tt(["pm1", "negI"], ["SH"], T.SH[:], T.pm1[:], T.negI[:], ALU.add)
+    cpv(["rli"], ["r1"], T.r1[:], T.rli[:])
+    mm(["E8T", "sgb"], ["pB"], T.pB[:, 0:C], T.E8T[0:8, :], T.sgb[0:8, :], True, True)
+    mm(["SH", "r1"], ["pA"], T.pA[:, 0:C], T.SH[:], T.r1[:], True, True)
+    cps(["pB"], ["r2"], T.r2[:], T.pB[:, 0:C])
+    ts(["pf"], ["pc7"], T.pc[:, 7:8], T.pf[:, 1:2], 15.0, ALU.is_lt)
+    cpv(["wi"], ["wf"], T.wf[:], T.wi[:])
+    ts(["pc0", "pc2", "pc3", "pc4", "pc5", "pc7"], ["pc"], T.pc[:, 6:7], T.pc[:, 2:3], T.pc[:, 7:8], ALU.mult)
+    ts(["colf", "pc0", "wf"], ["BW"], T.BW[:], T.colf[:], T.pc[:, 0:1], ALU.is_equal, T.wf[:, 0:1], ALU.mult)
+    ts(["colf"], ["ob"], T.ob[:], T.colf[:, 0:CD], 0.0, ALU.add)
+    ts(["colf", "pc"], ["onx"], T.onx[:], T.colf[:, 0:CD], 16.0, ALU.mult, T.pc[:, 6:7], ALU.add)
+    tt(["pA", "r2"], ["r3"], T.r3[:], T.pA[:, 0:C], T.r2[:], ALU.mult)
+    act(["colf", "ps2"], ["k1"], T.k1[:, 0:144], T.colf[:], ACT.Abs, T.ps[:, 2:3], 1.0)
+    act(["colm", "ps0"], ["k2"], T.k2[:], T.colm[:], ACT.Abs, T.ps[:, 0:1], 1.0)
+    act(["colf", "ps3"], ["k3"], T.k1[:, 144:152], T.colf[:, 0:8], ACT.Abs, T.ps[:, 3:4], 1.0)
+    act(["colm"], ["rs1"], T.rs1[:], T.colm[:], ACT.Relu, 1.0, -1.0)
+    act(["k1"], ["BE"], T.BE[:], T.k1[:, 0:144], ACT.Relu, 4096.0, -4096.0)
+    act(["k2"], ["diag"], T.diag[:], T.k2[:], ACT.Relu, 1.0, -1.0)
+    act(["k3"], ["E8"], T.E8[:], T.k1[:, 144:152], ACT.Relu, 1.0, -1.0)
+    act(["rs1"], ["rsn"], T.rsn[:], T.rs1[:], ACT.Identity, 0.0, -1e20)
+    act(["negI"], ["vI"], T.vI[:], T.negI[:], ACT.Identity, 0.0, BIG)
+    act(["colm", "ps1"], ["m8"], T.m8[:], T.colm[:], ACT.Relu, T.ps[:, 1:2], 8192.0)
+    tt(["r3", "r1"], ["r4"], T.r4[:], T.r3[:], T.r1[:], ALU.add)
+    turn(T.r4[:], ["r4"], T.Rf[:, 0:C], "Rf")
+    cpv(["Rf"], ["mi0"], T.mi0[:, 0:C], T.Rf[:, 0:C])
+    ts(["colf"], ["oc"], T.oc[:], T.colf[:, 0:CD], float(CD), ALU.add)
+    ts(["colf", "pc"], ["opa"], T.opa[:], T.colf[:, 0:CD], T.pc[:, 3:4], ALU.add)
+    ts(["colf", "pc"], ["opb"], T.opb[:], T.colf[:, 0:CD], T.pc[:, 3:4], ALU.add, float(CD), ALU.add)
+
+    def diagonal(name, src, B, bkey, out, okey, last):
+        def run(a, b, end):
+            for r in range(16):
+                mm(blocks(name, a, b) + [bkey], [okey], out[:, 16 * a:16 * b], B[:, 15 - r:143 - r],
+                   src[:, 256 * a + r:256 * b:16], False, end and r == 15)
+        return run
+
+    def peers(t):
+        hop = HOP if t < TS - 1 else -HOP * t
+        return T.cores[(rank + hop) % N], T.cores[(rank - hop) % N]
+
+    def levels(t):
+        ai, mo, ao = "ai%d" % t, "mo%d" % t, "ao%d" % t
+
+        def second():
+            tt(["ta", ai], [ao], T[ao][:], T.ta[:], T[ai][:], ALU.add)
+            send(ao, "ai%d" % (t + 1), "ra%d" % (t + 1), peers(t)[0])
+            expect("ai%d" % (t + 1), "ra%d" % (t + 1), peers(t)[1])
+        return [lambda: tt(["w01", mo, "c3"], ["ta"], T.ta[:], T.w01[:].indirect(T[mo][:, C:C + CD]), T.c3[:], ALU.mult),
+                second]
+
+    R = T.Rf[:, 0:C]
+
+    def arrive(t):
+        mi = "mi%d" % t
+        return [lambda: cpv([mi], ["Rf"], T.Rf[:], T[mi][:]),
+                lambda: ts(["Rf"], ["pD"], T.pD[:, C:2 * C], R, -HALF, ALU.add),
+                lambda: cpv(["Rf", "onx"], ["Rn"], T.Rn[:], R.indirect(T.onx[:])),
+                lambda: tt(["Rn", "pD"], ["i3"], T.i3[:], T.Rn[:], T.pD[:, C:2 * C], ALU.subtract)]
+
+    def in_order():
+        calls = [lambda: cpv(["mi%d" % TS], ["sa0", "sa1"], T.sa[:], T["mi%d" % TS][:, 0:C])]
+        for a, b in (("sa", "sb"), ("sb", "sa")) * 2:
+            for j, o in ((0, ALU.min), (1, ALU.max)):
+                calls.append(lambda a=a, b=b, j=j, o=o: tt([a + "0", a + "1"], [b + str(j)], T[b][:, :, j:16:2],
+                                                           T[a][:, :, 0:8], T[a][:, :, 8:16], o))
+        return calls
+
+    for f in arrive(0)[1:]:
+        f()
+    rest, later = [], []
+    for t in range(TS):
+        mi, ai, mo = "mi%d" % t, "ai%d" % t, "mo%d" % t
+        M, A = T[mi], T[ai]
+        dst, src = peers(t)
+
+        def gather_r(e, a, b):
+            f = cpv if e == "V" else cps
+            f(["X", mi], blocks("G", a, b), T.G[:, 256 * a:256 * b], XT.indirect(M[:, 16 * a:16 * b]))
+        wsum = diagonal("G", T.G, T.BW, "BW", T.pW, "pW", True)
+        if t > 0:
+            cps(["Rf", "ob"], ["gob"], T.gob[:], T.Rf[:, C:C + CD].indirect(T.ob[:]))
+            mm(["diag", "gob"], ["pN"], T.pN[:, 0:C], T.diag[:, 0:128], T.gob[:], True, True)
+            mm(["diag", "gob"], ["pW"], T.pW[:, 0:C], T.diag[:, 0:128], T.gob[:], True, False)
+        else:
+            mm(["zer"], ["pW"], T.pW[:, 0:C], T.zer[:, 0:128], T.zer[:], True, False)
+        for j in range(3):
+            gather_r("S", *R_S[j])
+            gather_r("V", *R_V[j])
+            wsum(PE_CH[j][0], PE_CH[j][1], j == 2)
+            if j == LATER:
+                for f in later:
+                    f()
+        for f in rest[FILL:]:
+            f()
+        mm(["negI", "Rf"], ["pK"], T.pK[:, 0:C], T.negI[:], R, True, False)
+        if t > 0:
+            cps(["pN"], ["nb"], T.nb[:], T.pN[:, 0:C])
+        ts(["i3"], ["i4"], T.i4[:], T.i3[:], W - 1, ALU.bitwise_and)
+        ts(["i4"], ["pD"], T.pD[:, 0:C], T.i4[:], 1.0 / 256, ALU.mult)
+
+        for a, b in AB_CH:
+            cps([ai], [("Ab", a)], T.Ab[:, a:b, 0:16], A[:, 16 * a:16 * b])
+            for n in (16, 32, 64):
+                cps([("Ab", a)], [("Ab", a)], T.Ab[:, a:b, n:2 * n], T.Ab[:, a:b, 0:n])
+            cps([("Ab", a)], blocks("Ab", a, b), T.Ab[:, a:b, 128:256], T.Ab[:, a:b, 0:128])
+
+        if t > 0:
+            tt(["pW", "nb"], ["i1"], T.i1[:], T.pW[:, 0:C], T.nb[:], ALU.subtract)
+        else:
+            cpv(["pW"], ["i1"], T.i1[:], T.pW[:, 0:C])
+        ts(["i1"], ["u0"], T.u[:, :, 0:16], T.i1[:], W - 1, ALU.bitwise_and)
+        ts(["i1"], ["u1"], T.u[:, :, 16], T.i1[:, 0:C:16], W - 1, ALU.bitwise_and)
+        tt(["u0", "u1"], ["i2"], T.i2[:], T.u[:, :, 0:16], T.u[:, :, 1:17], ALU.mult)
+        ts(["i2"], ["i1"], T.i1[:], T.i2[:], 5, ALU.logical_shift_right)
+        tt(["i1", "pW"], ["i2"], T.i2[:], T.pW[:, 0:C], T.i1[:], ALU.add)
+        ts(["i2"], ["i1"], T.i1[:], T.i2[:], 255, ALU.bitwise_and)
+        tt(["i1", "pD"], ["dh"], T.dh[:], T.pD[:, 0:C], T.i1[:], ALU.mult)
+        tt(["dh", "pD"], ["i2"], T.i2[:], T.pD[:, C:2 * C], T.dh[:], ALU.add)
+        ts(["i2"], ["qi"], T.qi[:], T.i2[:], W - 1, ALU.bitwise_and)
+        cpv(["qi"], ["qu"], T.qu[:], T.qi[:])
+        op("S", ["dh"], ["vo"], lambda: g.scalar.activation(T.vo[:], T.dh[:], ACT.Relu, bias=256.0, scale=-256.0))
+        mm(["vI", "vo"], ["pK"], T.pK[:, 0:C], T.vI[:], T.vo[:], False, False)
+        cps(["Rf"], ["Yl1"], T.Yl[:, CD:2 * CD], T.Rf[:, 0:C:16])
+        cps(["Rf"], ["Yl2"], T.Yl[:, 2 * CD:3 * CD], T.Rf[:, 15:C:16])
+
+        esum = diagonal("DA", T.DA, T.BE, "BE", T.pK, "pK", True)
+        done = 0
+        for a, b in Q_CH:
+            for cd in range(a, b):
+                tt(["X", "qu", ("Ab", cd)], [("D", cd)], T.D[:, 256 * cd:256 * cd + 256],
+                   XT.indirect(T.qu[:, 16 * cd:16 * cd + 16]), T.Ab[:, cd, :], ALU.subtract)
+            op("S", blocks("D", a, b), blocks("DA", a, b),
+               lambda: g.scalar.activation(T.DA[:, 256 * a:256 * b], T.D[:, 256 * a:256 * b], ACT.Abs))
+            while done < len(PE_CH) and PE_CH[done][1] <= b:
+                esum(PE_CH[done][0], PE_CH[done][1], done == len(PE_CH) - 1)
+                done += 1
+        tt(["qi", "DY"], ["DY0"], T.DY[:, 1:C], T.qi[:, 0:C - 1], T.qi[:, 1:C], ALU.subtract)
+        tt(["Rf", "Rn", "DY"], ["DY1"], T.DY[:, C + 1:2 * C:2], T.Rf[:, 0:C:2], T.Rn[:, 1:C:2], ALU.subtract)
+        tt(["Rf", "Rn", "DY"], ["DY2"], T.DY[:, 2 * C + 2:3 * C:2], T.Rf[:, 1:C - 1:2], T.Rn[:, 2:C:2], ALU.subtract)
+        cpv(["qi"], ["Yl0"], T.Yl[:, 0:CD], T.qi[:, 15:C:16])
+        scan(["rsn", "pK"], ["run"], T.run[:], T.rsn[:], T.pK[:, 0:C], ALU.add, ALU.max)
+        tt(["pK", "run"], ["nn"], T.nn[:], T.pK[:, 0:C], T.run[:], ALU.not_equal)
+        for j in range(3):
+            scan(["DY%d" % j, "DY", "nn"], ["wy%d" % j], T.wy[:, j * C:(j + 1) * C], T.DY[:, j * C:(j + 1) * C], T.nn[:],
+                 ALU.add, ALU.mult)
+        cps(["run"], ["Kx0"], T.Kx[:, 0:CD], T.run[:, 15:C:16])
+        cps(["run"], ["Kx1"], T.Kx[:, CD:2 * CD], T.run[:, 15:C:16])
+        tt(["wy0", "wy1", "wy2", "Yl0", "Yl1", "Yl2"], ["Yb"], T.Yb[:], T.wy[:, 15:3 * C:16], T.Yl[:], ALU.add)
+        cpv(["Yb"], ["o3"], T.o3[:], T.Yb[:])
+
+        for j in (1, 2, 0):
+            tt(["X", "o3", ai], [("D3", j)], T.D3[:, j * C:(j + 1) * C], XT.indirect(T.o3[:, j * CD:(j + 1) * CD]), A[:],
+               ALU.subtract)
+            if j:
+                op("S", [("D3", j)], [("T3", j)],
+                   lambda: g.scalar.activation(T.T3[:, (j - 1) * C:j * C], T.D3[:, j * C:(j + 1) * C], ACT.Abs))
+        ts([("D3", 0)], [("T3", 0)], T.T3[:, 2 * C:3 * C], T.D3[:, 0:C], 0.0, ALU.is_le)
+        for r in range(16):
+            mm(blocks("T3", 0, 3) + ["BE"], ["p3"], T.p3[:, 0:3 * CD], T.BE[:, 15 - r:143 - r], T.T3[:, r:3 * C:16],
+               r == 0, r == 15)
+        tt(["Yb", "opb", "Rf"], ["mm"], T.mm[:], T.Yb[:].indirect(T.opb[:]), R, ALU.is_equal)
+        tt(["Yb"], ["dl0"], T.dl[:, 0:CD], T.Yb[:, 0:CD], T.Yb[:, CD:2 * CD], ALU.subtract)
+        tt(["Yb"], ["dl1"], T.dl[:, CD:2 * CD], T.Yb[:, 0:CD], T.Yb[:, 2 * CD:3 * CD], ALU.subtract)
+        ts(["Yb"], ["ee"], T.ee[:], T.Yb[:, CD:3 * CD], float(PAD), ALU.add)
+        ts([("D3", 0)], ["c3"], T.c3[:], T.D3[:, 0:C], -3.0, ALU.max, 3.0, ALU.min)
+        tt(["p3", "Kx0", "Kx1", "Kx2"], ["F"], T.F[:], T.p3[:, 0:3 * CD], T.Kx[:], ALU.is_lt)
+        tt(["F"], ["gg0"], T.gg[:, 0:CD], T.F[:, 0:CD], T.F[:, 2 * CD:3 * CD], ALU.mult)
+        tt(["F"], ["gg1"], T.gg[:, CD:2 * CD], T.F[:, CD:2 * CD], T.F[:, 2 * CD:3 * CD], ALU.is_gt)
+        tt(["gg0", "gg1", "dl0", "dl1"], ["dg"], T.dg[:], T.gg[:], T.dl[:], ALU.mult)
+        KA, KU = T.MF[:, C + CD:C + 2 * CD], T[mo][:, C + CD:C + 2 * CD]
+        tt(["gg0", "gg1", "ee"], ["te"], T.te[:], T.gg[:], T.ee[:], ALU.mult)
+        tt(["dg", "opa", "mm"], ["rr"], T.rr[:], T.dg[:].indirect(T.opa[:]), T.mm[:], ALU.mult)
+        tt(["gg0", "gg1"], ["MF1"], T.MF[:, C:C + CD], T.gg[:, 0:CD], T.gg[:, CD:2 * CD], ALU.add)
+        tt(["te"], ["ka"], KA, T.te[:, 0:CD], T.te[:, CD:2 * CD], ALU.add)
+        tt(["rr", "pD"], ["MF0"], T.MF[:, 0:C], T.pD[:, C:2 * C], T.rr[:], ALU.add)
+        ts(["MF0", "MF1", "ka"], [mo], T[mo][:], T.MF[:], HALF, ALU.add)
+        send(mo, "mi%d" % (t + 1), "rm%d" % (t + 1), dst)
+        expect("mi%d" % (t + 1), "rm%d" % (t + 1), src)
+        rest = arrive(t + 1) if t < TS - 1 else in_order()
+        now, later = (levels(t), []) if LATER < 0 or t == TS - 1 else ([None, None], levels(t))
+        fill = now + [None] * (CD - 2 - FILL) + rest[:FILL]
+
+        tt(["IOT", mo, "m8"], ["Nm"], T.Nm[:], T.IOT[:].indirect(KU), T.m8[:], ALU.add)
+        act(["X", "Xpad", mo], ["xl"], T.xl[:], T.X[:].indirect(KU), ACT.Identity, -5.0, 1.0)
+        tt(["X", "Xpad", mo, ai], ["dx"], T.dx[:], T.X[:].indirect(KU), A[:], ALU.subtract)
+        act(["dx"], ["c4"], T.c4[:], T.dx[:], ACT.Relu, 5.0, 1.0)
+        act(["c4"], ["c5"], T.c5[:], T.c4[:], ACT.Relu, 10.0, -1.0)
+        tt(["ka", "MF1", "oc", "Nm"], ["ne"], T.ne[:], T.MF[:, C:C + 2 * CD].indirect(T.oc[:]), T.Nm[:], ALU.not_equal)
+        scan(["rs1", "ne"], ["nd"], T.nd[:], T.rs1[:], T.ne[:], ALU.max, ALU.min)
+        tt(["ka", "nd"], ["kn"], T.kn[:], KA, T.nd[:, 15:C:16], ALU.mult)
+        if fill[0] is not None:
+            fill[0]()
+        ts(["kn", "pc"], ["lo"], T.lo[:, 0:2 * CD:2], T.kn[:], T.pc[:, 2:3], ALU.max)
+        for cd in range(CD - 1, -1, -1):
+            tt(["lo", "xl", "c5"], ["X", "Xpad"], T.X[:].indirect(T.lo[:, 2 * cd:2 * cd + 1]),
+               T.xl[:, 16 * cd:16 * cd + 16], T.c5[:, 16 * cd:16 * cd + 16], ALU.add)
+            if cd > 0 and fill[CD - cd] is not None:
+                fill[CD - cd]()
+
+    dma("Y", "ox", ["X"], [], T.yx[:], XT)
+    mi, ai = "mi%d" % TS, "ai%d" % TS
+    dma("S", "oa", [ai], [], T.ya[:], T[ai][:])
+    for f in rest[FILL:]:
+        f()
+    a, b = "sa", "sb"
+    turn(T[a][:], [a + "0", a + "1"], T.r1[:], "r1")
+    dma("Y", "orr", ["r1"], [], T.yr[:], T.r1[:])
+    tt([b + "0", b + "1"], ["sf"], T.sf[:, 0:CD], T[b][:, :, 0], T[b][:, :, 8], ALU.is_lt)
+    tt(["sf", "ob", "diag"], ["sx"], T.sx[:], T.sf[:].indirect(T.ob[:]), T.diag[:], ALU.mult)
+    mm(["E8", "sx"], ["pA"], T.pA[0:8, 0:C], T.E8[:], T.sx[:], True, True)
+    act(["pA"], ["so"], T.so[0:8, :], T.pA[0:8, 0:C], ACT.Identity, -1.0, 2.0)
+    dma("S", "osg", ["so"], [], T.ys[:], T.so[0:8, :])
+    for s, v in final.items():
+        wait("G", s, v)

@@ -1,75 +1,43 @@
-from concourse.bass import DstId, RemoteDMATransfer
-from concourse.mybir import dt, AluOpType, AxisListType, ActivationFunctionType
+from concourse.mybir import AluOpType, ActivationFunctionType
 
 ALU = AluOpType
 ACT = ActivationFunctionType
 W, C, TS, HOP = 4096, 192, 5, 3
 CD = C // 16
-PAD = 32
+H, HD = C // 2, CD // 2
+PAD = 48
 BIG = 16777216.0
+HALF = 255.0 / 512
+F32, BF, I32, U16 = "float32", "bfloat16", "int32", "uint16"
 
-SCRATCH = {
-    "X": ("sbuf", [128, W + PAD], "bfloat16"), "IOT": ("sbuf", [128, W + PAD], "float32"),
-    "G": ("sbuf", [128, 16 * C], "bfloat16"), "D": ("sbuf", [128, 16 * C], "bfloat16"),
-    "DA": ("sbuf", [128, 16 * C], "bfloat16"), "Ab": ("sbuf", [128, CD, 256], "bfloat16"),
-    "ti": ("sbuf", [128, 8], "int32"), "pf": ("sbuf", [128, 8], "float32"), "pc": ("sbuf", [128, 8], "float32"),
-    "wi": ("sbuf", [128, 1], "int32"), "wf": ("sbuf", [128, 1], "float32"),
-    "cp": ("sbuf", [128, 128], "float32"), "colm": ("sbuf", [128, C], "float32"), "colf": ("sbuf", [128, 144], "float32"),
-    "chi": ("sbuf", [128, 128], "float32"),
-    "negI": ("sbuf", [128, 128], "float32"), "vI": ("sbuf", [128, 128], "bfloat16"), "SH": ("sbuf", [128, 128], "float32"),
-    "pm1": ("sbuf", [128, 128], "float32"), "ps": ("sbuf", [128, 4], "float32"),
-    "k1": ("sbuf", [128, 152], "float32"), "k2": ("sbuf", [128, C], "float32"),
-    "diag": ("sbuf", [128, C], "bfloat16"), "m8": ("sbuf", [128, C], "float32"), "rsn": ("sbuf", [128, C], "float32"),
-    "rs1": ("sbuf", [128, C], "float32"), "BW": ("sbuf", [128, 144], "bfloat16"), "BE": ("sbuf", [128, 144], "bfloat16"),
-    "E8T": ("sbuf", [128, 128], "bfloat16"), "E8": ("sbuf", [128, 8], "bfloat16"), "zer": ("sbuf", [128, C], "bfloat16"),
-    "w01": ("sbuf", [128, 16], "bfloat16"),
-    "ob": ("sbuf", [128, CD], "uint16"), "opa": ("sbuf", [128, CD], "uint16"), "opb": ("sbuf", [128, CD], "uint16"),
-    "onx": ("sbuf", [128, CD], "uint16"),
-    "rli": ("sbuf", [128, C], "int32"), "sgi": ("sbuf", [128, C], "int32"), "sgb": ("sbuf", [128, C], "bfloat16"),
-    "r1": ("sbuf", [128, C], "float32"), "r2": ("sbuf", [128, C], "float32"), "r3": ("sbuf", [128, C], "float32"),
-    "r4": ("sbuf", [128, C], "float32"),
-    "Z": ("sbuf", [128, CD, 32], "float32"), "Zt": ("sbuf", [128, CD, 32], "float32"),
-    "sa": ("sbuf", [128, CD, 16], "float32"), "sb": ("sbuf", [128, CD, 16], "float32"),
-    "sf": ("sbuf", [128, 16], "float32"), "sx": ("sbuf", [128, C], "bfloat16"), "so": ("sbuf", [128, C], "float32"),
-    "Rf": ("sbuf", [128, C + CD], "float32"), "MF": ("sbuf", [128, C + 2 * CD], "float32"), "Rn": ("sbuf", [128, C], "float32"),
-    "gob": ("sbuf", [128, C], "bfloat16"), "nb": ("sbuf", [128, C], "float32"),
-    "i1": ("sbuf", [128, C], "int32"), "i2": ("sbuf", [128, C], "int32"), "i3": ("sbuf", [128, C], "int32"),
-    "i4": ("sbuf", [128, C], "int32"), "u": ("sbuf", [128, CD, 17], "int32"), "dh": ("sbuf", [128, C], "float32"),
-    "qi": ("sbuf", [128, C], "int32"), "qu": ("sbuf", [128, C], "uint16"), "vo": ("sbuf", [128, C], "bfloat16"),
-    "DY": ("sbuf", [128, 3 * C], "float32"), "wy": ("sbuf", [128, 3 * C], "float32"), "Yl": ("sbuf", [128, 3 * CD], "float32"),
-    "Yb": ("sbuf", [128, 3 * CD], "float32"), "o3": ("sbuf", [128, 3 * CD], "uint16"), "run": ("sbuf", [128, C], "float32"),
-    "nn": ("sbuf", [128, C], "float32"), "Kx": ("sbuf", [128, 3 * CD], "float32"), "D3": ("sbuf", [128, 3 * C], "bfloat16"),
-    "T3": ("sbuf", [128, 3 * C], "bfloat16"), "F": ("sbuf", [128, 3 * CD], "float32"), "gg": ("sbuf", [128, 2 * CD], "float32"),
-    "dl": ("sbuf", [128, 2 * CD], "float32"), "dg": ("sbuf", [128, 2 * CD], "float32"), "ee": ("sbuf", [128, 2 * CD], "float32"),
-    "te": ("sbuf", [128, 2 * CD], "float32"), "oc": ("sbuf", [128, CD], "uint16"),
-    "mm": ("sbuf", [128, C], "float32"), "rr": ("sbuf", [128, C], "float32"), "c3": ("sbuf", [128, C], "bfloat16"),
-    "ta": ("sbuf", [128, C], "bfloat16"), "Nm": ("sbuf", [128, C], "float32"), "ne": ("sbuf", [128, C], "float32"),
-    "nd": ("sbuf", [128, C], "float32"), "kn": ("sbuf", [128, CD], "float32"), "lo": ("sbuf", [128, 2 * CD], "uint16"),
-    "xl": ("sbuf", [128, C], "bfloat16"), "dx": ("sbuf", [128, C], "bfloat16"), "c5": ("sbuf", [128, C], "bfloat16"),
-    "c4": ("sbuf", [128, C], "bfloat16"),
-    "pW": ("psum", [128, 512], "float32"), "pK": ("psum", [128, 512], "float32"), "p3": ("psum", [128, 512], "float32"),
-    "pN": ("psum", [128, 512], "float32"), "pD": ("psum", [128, 512], "float32"), "pA": ("psum", [128, 512], "float32"),
-    "pB": ("psum", [128, 512], "float32"),
-}
-for _t in range(TS + 1):
-    SCRATCH["mi%d" % _t] = ("sbuf", [128, C + CD], "uint16")
-    SCRATCH["ai%d" % _t] = ("sbuf", [128, C], "bfloat16")
-for _t in range(TS):
-    SCRATCH["mo%d" % _t] = ("sbuf", [128, C + 2 * CD], "uint16")
-    SCRATCH["ao%d" % _t] = ("sbuf", [128, C], "bfloat16")
+SCRATCH = {"Ab": ("sbuf", [128, CD, 256], BF), "u": ("sbuf", [128, CD, 17], I32), "Yb": ("sbuf", [128, 3, CD], F32),
+           "Z": ("sbuf", [128, CD, 32], F32), "Zt": ("sbuf", [128, CD, 32], F32),
+           "sa": ("sbuf", [128, CD, 16], F32), "sb": ("sbuf", [128, CD, 16], F32)}
+for _names, _n, _d in (
+        ("X", W + PAD, BF), ("IOT", W + PAD, F32), ("G D DA", 16 * C, BF),
+        ("ti", 8, I32), ("pf pc", 8, F32), ("ps", 5, F32), ("oc", HD, U16), ("Ne n2 n3", H, F32), ("cand", C, F32),
+        ("ka", CD + HD, F32), ("ku", CD + HD, U16), ("kb", CD, F32), ("wi", 1, I32), ("wf", 1, F32),
+        ("cp chi negI SH pm1", 128, F32), ("vI E8T", 128, BF), ("colf", 144, F32), ("k1", 152, F32), ("BW BE", 144, BF),
+        ("E8", 8, BF), ("w01", 16, BF), ("sf", 16, F32), ("ob opa onx lo", CD, U16),
+        ("colm k2 m8 rsn rs1 r1 r2 r3 so Rn nb dh run nn mm rr Nm ne nd", C, F32),
+        ("diag zer sgb sx gob vo c3 ta xl dx c4 c5", C, BF), ("rli sgi i1 i2 i3 i4 qi", C, I32), ("qu", C, U16),
+        ("Rf MF", C + CD, F32), ("DY wy", 3 * C, F32), ("D3 T3", 3 * C, BF),
+        ("Yl Kx F", 3 * CD, F32), ("o3", 3 * CD, U16), ("gg dl ee te rp", 2 * CD, F32), ("kn", CD, F32),
+        ("mi0 mi1 mi2 mi3 mi4 mi5", C + CD, U16),
+        ("mo0 mo1 mo2 mo3 mo4", C + CD, U16),
+        ("ai0 ai1 ai2 ai3 ai4 ai5 ao0 ao1 ao2 ao3 ao4", C, BF)):
+    for _x in _names.split():
+        SCRATCH[_x] = ("sbuf", [128, _n], _d)
+PSUM = ("pW", "pK", "p3", "pN", "pA", "pB")
+for _x in PSUM + ("pD",):
+    SCRATCH[_x] = ("psum", [128, 512], F32)
 
 SEMAPHORES = (["cV", "cS", "cP", "cG", "sent", "lx", "lr", "la", "ls", "lw", "ox", "oa", "orr", "osg"]
               + ["rm%d" % t for t in range(1, TS + 1)] + ["ra%d" % t for t in range(1, TS + 1)])
-PSUM = ("pW", "pK", "p3", "pN", "pD", "pA", "pB")
 
-HALF = 255.0 / 512
-R_V = [(0, 2), (4, 6), (8, 9)]
-R_S = [(2, 4), (6, 8), (9, 12)]
-FILL = 1
-LATER = 0
-Q_CH = [(0, 2), (2, 4), (4, 6), (6, 8), (8, 10), (10, 11), (11, 12)]
-PE_CH = [(0, 4), (4, 8), (8, 12)]
-AB_CH = [(0, 6), (6, 12)]
+R_CH = [("V", 0, 3), ("S", 3, 6), ("V", 6, 8), ("S", 8, 12)]
+ABS_CH = [(0, 2), (2, 4), (4, 6), (6, 8), (8, 10), (10, 11), (11, 12)]
+CYCLE, PE_CYCLE, WAKE, SLACK, FLIGHT = 0.9, 0.8, 140.0, 20.0, 3500.0
 
 
 def rank_program(g, core, T, topo):
@@ -78,56 +46,102 @@ def rank_program(g, core, T, topo):
         return
     N = len(T.cores)
     Q = {"V": g.vector, "S": g.scalar, "P": g.tensor, "G": g, "Y": g.sync}
-    count = {"V": 0, "S": 0, "P": 0, "G": 0}
-    known = {}
+    ops = []
     writer = {}
     readers = {}
-    final = {}
 
-    def wait(e, sem, val):
-        if known.get((e, sem), 0) < val:
-            known[(e, sem)] = val
-            Q[e].wait_ge(T.sem[sem], val)
-
-    def order(e, reads, writes):
-        need = {}
-        for k in reads:
+    def add(e, reads, writes, call, cost, lat=0.0, sem=None, inc=1):
+        deps = set()
+        for k in list(reads) + list(writes):
             if k in writer:
-                s, v, we = writer[k]
-                if not (e == "P" and we == "P"):
-                    need[s] = max(need.get(s, 0), v)
-        for k in list(writes) + [k for k in reads if k in PSUM]:
-            if k in writer and not (e == "P" and writer[k][2] == "P"):
-                s, v, we = writer[k]
-                need[s] = max(need.get(s, 0), v)
-            for oe, (s, v) in readers.get(k, {}).items():
-                if oe != e or k in writes:
-                    need[s] = max(need.get(s, 0), v)
-        for s, v in need.items():
-            wait(e, s, v)
-
-    def note(e, sem, val, reads, writes):
+                deps.add(writer[k])
         for k in writes:
-            writer[k] = (sem, val, e)
-            readers[k] = {}
+            deps.update(readers.get(k, []))
+        for k in reads:
+            if k in PSUM:
+                deps.update(i for i in readers.get(k, []) if ops[i]["e"] != e)
+        ops.append({"e": e, "deps": deps, "call": call, "cost": cost, "lat": lat, "sem": sem, "inc": inc, "soft": set()})
+        for k in writes:
+            writer[k] = len(ops) - 1
+            readers[k] = []
         for k in reads:
             if k not in writes:
-                readers.setdefault(k, {})[e] = (sem, val)
-        final[sem] = val
+                readers.setdefault(k, []).append(len(ops) - 1)
 
-    def op(e, reads, writes, call):
-        order(e, reads, writes)
-        count[e] += 1
-        call().then_inc(T.sem["c" + e], 1)
-        note(e, "c" + e, count[e], reads, writes)
+    def behind(*keys):
+        o = ops[-1]
+        o["soft"] = {writer[k] for k in keys if k in writer and ops[writer[k]]["e"] == o["e"]} - o["deps"] - {len(ops) - 1}
+        o["deps"] = o["deps"] | o["soft"]
+
+    def emit():
+        n = len(ops)
+        after = [[] for _ in range(n)]
+        for i, o in enumerate(ops):
+            for d in o["deps"]:
+                after[d].append(i)
+
+        def gap(d, i):
+            if d in ops[i]["soft"] or (ops[d]["e"] == "P" and ops[i]["e"] == "P"):
+                return 0.0
+            return ops[d]["lat"] + WAKE
+        tail = [0.0] * n
+        for i in range(n - 1, -1, -1):
+            tail[i] = ops[i]["cost"] + max([gap(i, j) + tail[j] for j in after[i]] + [ops[i]["lat"]])
+        left = [len(o["deps"]) for o in ops]
+        ready_at = [0.0] * n
+        ready = [i for i in range(n) if left[i] == 0]
+        free, known, final, mark = {}, {}, {}, {}
+        while ready:
+            start = {i: max(ready_at[i], free.get(ops[i]["e"], 0.0)) for i in ready}
+            first = min(ready, key=lambda i: (start[i], -tail[i], i))
+            e = ops[first]["e"]
+            i = max((j for j in ready if ops[j]["e"] == e and start[j] <= start[first] + SLACK), key=lambda j: (tail[j], -j))
+            o = ops[i]
+            ready.remove(i)
+            end = start[i] + o["cost"]
+            s = o["sem"] or "c" + e
+            final[s] = final.get(s, 0) + o["inc"]
+            mark[i] = (s, final[s])
+            if e != "F":
+                free[e] = end
+                need = {}
+                for d in o["deps"] - o["soft"]:
+                    if not (e == "P" and ops[d]["e"] == "P"):
+                        need[mark[d][0]] = max(need.get(mark[d][0], 0), mark[d][1])
+                for w, v in need.items():
+                    if known.get((e, w), 0) < v:
+                        known[(e, w)] = v
+                        Q[e].wait_ge(T.sem[w], v)
+                done = o["call"]()
+                if s != "sent":
+                    done.then_inc(T.sem[s], o["inc"])
+            for j in after[i]:
+                ready_at[j] = max(ready_at[j], end + gap(i, j))
+                left[j] -= 1
+                if left[j] == 0:
+                    ready.append(j)
+        for s, v in final.items():
+            g.wait_ge(T.sem[s], v)
+
+    def size(ap):
+        n = 1
+        for x in ap.shape[1:]:
+            n *= x
+        return n
+
+    def price(out, per, kind=None):
+        if kind == "scatter":
+            return 50.0 + 32 * 3.8 * CYCLE
+        if kind == "gather":
+            return 50.0 + size(out) * 1.56 * CYCLE
+        return 60.0 + max(64, size(out) * per) * CYCLE
 
     def dma(e, sem, reads, writes, out, in_, slow=False):
-        order(e, reads, writes)
-        if slow:
-            Q[e].dma_start(out, in_, allow_slow_non_contiguous=True).then_inc(T.sem[sem], 16)
-        else:
-            Q[e].dma_start(out, in_).then_inc(T.sem[sem], 16)
-        note("dma" + sem, sem, final.get(sem, 0) + 16, reads, writes)
+        def call():
+            if slow:
+                return Q[e].dma_start(out, in_, allow_slow_non_contiguous=True)
+            return Q[e].dma_start(out, in_)
+        add(e, reads, writes, call, 100.0, 2000.0 + 1.3 * size(out), sem, 16)
 
     def lanes(src, dst):
         m = 0
@@ -136,75 +150,81 @@ def rank_program(g, core, T, topo):
             m |= 1 << x
         return m, len(es)
 
-    def send(name, dst_name, sem, dst):
-        order("G", [name], [])
+    def send(name, there, sem, t):
+        hop = HOP if t < TS - 1 else -HOP * t
+        dst, src = T.cores[(rank + hop) % N], T.cores[(rank - hop) % N]
         rid, pid, _ = topo.addr(dst)
         m, n = lanes(core, dst)
-        g.remote_dma(T[dst_name][:], T[name][:, 0:T[dst_name].shape[1]], T.sem[sem], T.sem.sent, pid, rid, m)
-        final["sent"] = final.get("sent", 0) + n
+        add("G", [name], ["sent " + name],
+            lambda: g.remote_dma(T[there][:], T[name][:, 0:T[there].shape[1]], T.sem[sem], T.sem.sent, pid, rid, m),
+            500.0, 0.0, "sent", n)
+        add("F", ["sent " + name], [there], None, FLIGHT, 0.0, sem, lanes(src, core)[1])
 
-    def expect(name, sem, src):
-        n = lanes(src, core)[1]
-        writer[name] = (sem, n, "far")
-        final[sem] = n
-
-    def tt(r, w, out, a, b, o):
-        op("V", r, w, lambda: g.vector.tensor_tensor(out, a, b, o))
+    def tt(r, w, out, a, b, o, kind=None):
+        both = 1 if any(k in PSUM or k in ("pD0", "pD1") for k in r) else 2
+        add("V", r, w, lambda: g.vector.tensor_tensor(out, a, b, o), price(out, both, kind))
 
     def ts(r, w, out, a, s1, o1, s2=None, o2=None):
         if o2 is None:
-            op("V", r, w, lambda: g.vector.tensor_scalar(out, a, s1, None, o1))
+            add("V", r, w, lambda: g.vector.tensor_scalar(out, a, s1, None, o1), price(out, 1))
         else:
-            op("V", r, w, lambda: g.vector.tensor_scalar(out, a, s1, s2, o1, o2))
+            add("V", r, w, lambda: g.vector.tensor_scalar(out, a, s1, s2, o1, o2), price(out, 1))
 
-    def cpv(r, w, out, a):
-        op("V", r, w, lambda: g.vector.tensor_copy(out, a))
+    def cpv(r, w, out, a, kind=None):
+        add("V", r, w, lambda: g.vector.tensor_copy(out, a), price(out, 1, kind))
 
-    def cps(r, w, out, a):
-        op("S", r, w, lambda: g.scalar.activation(out, a, ACT.Copy))
+    def cps(r, w, out, a, kind=None):
+        add("S", r, w, lambda: g.scalar.activation(out, a, ACT.Copy), price(out, 1, kind))
 
-    def act(r, w, out, a, func, bias, scale):
-        op("S", r, w, lambda: g.scalar.activation(out, a, func, bias=bias, scale=scale))
+    def act(r, w, out, a, func, bias, scale, kind=None):
+        add("S", r, w, lambda: g.scalar.activation(out, a, func, bias=bias, scale=scale), price(out, 1, kind))
 
     def mset(w, out, val):
-        op("V", [], w, lambda: g.vector.memset(out, val))
+        add("V", [], w, lambda: g.vector.memset(out, val), price(out, 0.5))
 
     def scan(r, w, out, d0, d1, o0, o1):
-        op("V", r, w, lambda: g.vector.tensor_tensor_scan(out, d0, d1, 0.0, o0, o1))
+        add("V", r, w, lambda: g.vector.tensor_tensor_scan(out, d0, d1, 0.0, o0, o1), price(out, 1))
 
-    def mm(r, w, out, lhsT, rhs, start, stop):
-        op("P", r, w, lambda: g.tensor.matmul(out, lhsT, rhs, start, stop))
+    def mm(r, w, out, lhsT, rhs, start, stop, wide=1):
+        add("P", r, w, lambda: g.tensor.matmul(out, lhsT, rhs, start, stop), max(64, size(out)) * wide * PE_CYCLE)
 
     def iota(w, out, pattern, base, mult):
-        op("G", [], w, lambda: g.iota(out, pattern, base, mult, allow_small_or_imprecise_dtypes=True))
+        add("G", [], w, lambda: g.iota(out, pattern, base, mult, allow_small_or_imprecise_dtypes=True),
+            130.0 + 2 * size(out) * CYCLE)
 
     def blocks(name, a, b):
         return [(name, i) for i in range(a, b)]
 
     def turn(src, src_keys, dst, dst_key):
-        ts(src_keys + ["pc"], ["Z0"], T.Z[:, :, 0:16], src, T.pc[:, 4:5], ALU.mult)
+        ts(src_keys + ["pc4"], ["Z0"], T.Z[:, :, 0:16], src, T.pc[:, 4:5], ALU.mult)
         ts(src_keys + ["pf"], ["Z1"], T.Z[:, :, 16:32], src, T.pf[:, 3:4], ALU.mult)
-        op("V", ["Z0", "Z1"], ["Zt"], lambda: g.vector.transpose(T.Zt[:], T.Z[:]))
+        add("V", ["Z0", "Z1"], ["Zt"], lambda: g.vector.transpose(T.Zt[:], T.Z[:]), price(T.Zt[:], 1))
         tt(["Zt"], [dst_key], dst, T.Zt[:, :, 0:16], T.Zt[:, :, 16:32], ALU.add)
 
+    def diagonal(name, B, out, a, b):
+        for r in range(16):
+            mm(blocks(name, a, b) + [B], [out], T[out][:, 0:16 * (b - a)], T[B][:, 15 - r:143 - r],
+               T[name][:, 256 * a + r:256 * b:16], False, r == 15)
+
     XT = T.X[:, PAD:PAD + W]
+    R = T.Rf[:, 0:C]
 
     dma("S", "lr", [], ["rli"], T.rli[:], T.rl[:])
     dma("Y", "ls", [], ["sgi"], T.sgi[0:8, :], T.sg[:])
     dma("Y", "lx", [], ["X"], XT, T.xt[:])
-    dma("Y", "la", [], ["ai0"], T.ai0[:], T.av[:])
-    op("G", [], ["ti0"], lambda: g.iota(T.ti[:, 0:1], [[0, 1]], 0, 1))
+    dma("S", "la", ["pf"], ["ai0"], T.ai0[:], T.av[:])
+    dma("G", "lw", ["cp"], ["wi"], T.wi[:], T.wt[:], slow=True)
+    add("G", [], ["ti0"], lambda: g.iota(T.ti[:, 0:1], [[0, 1]], 0, 1), 130.0)
     iota(["colf"], T.colf[:], [[1, 144]], 0, 0)
     iota(["cp"], T.cp[:], [[1, 128]], 0, -1)
     iota(["chi"], T.chi[0:8, :], [[1, 8], [0, 16]], 0, -1)
-    dma("G", "lw", [], ["wi"], T.wi[:], T.wt[:], slow=True)
     iota(["colm"], T.colm[:], [[0, CD], [1, 16]], 0, 0)
     iota(["DY"], T.DY[:], [[0, 3 * C]], 0, 0)
     iota(["Kx2"], T.Kx[:, 2 * CD:3 * CD], [[0, CD]], 17 * 2048, 0)
     iota(["w01"], T.w01[:], [[1, 16]], 0, 0)
     iota(["sf"], T.sf[:], [[0, 16]], 0, 0)
     iota(["IOT"], T.IOT[:], [[1, W + PAD]], 0, 0)
-
+    behind("ti0", "colf", "cp", "chi", "colm", "DY", "Kx2", "w01", "sf")
     mset(["Xpad"], T.X[:, 0:PAD], 0.0)
     mset(["zer"], T.zer[:], 0.0)
     ts(["ti0"], ["ti1"], T.ti[:, 1:2], T.ti[:, 0:1], 15, ALU.bitwise_and)
@@ -225,19 +245,16 @@ def rank_program(g, core, T, topo):
     act(["pf"], ["ps1"], T.ps[:, 1:2], T.pf[:, 1:2], ACT.Identity, 8192.0, -8192.0)
     act(["pf"], ["ps2"], T.ps[:, 2:3], T.pf[:, 2:3], ACT.Identity, -15.0, -16.0)
     act(["pf"], ["ps3"], T.ps[:, 3:4], T.pf[:, 2:3], ACT.Identity, 0.0, -1.0)
-    ts(["sgi"], ["sgb"], T.sgb[0:8, :], T.sgi[0:8, :], 0.0, ALU.is_lt)
     tt(["pm1", "negI"], ["SH"], T.SH[:], T.pm1[:], T.negI[:], ALU.add)
-    cpv(["rli"], ["r1"], T.r1[:], T.rli[:])
-    mm(["E8T", "sgb"], ["pB"], T.pB[:, 0:C], T.E8T[0:8, :], T.sgb[0:8, :], True, True)
-    mm(["SH", "r1"], ["pA"], T.pA[:, 0:C], T.SH[:], T.r1[:], True, True)
-    cps(["pB"], ["r2"], T.r2[:], T.pB[:, 0:C])
     ts(["pf"], ["pc7"], T.pc[:, 7:8], T.pf[:, 1:2], 15.0, ALU.is_lt)
     cpv(["wi"], ["wf"], T.wf[:], T.wi[:])
-    ts(["pc0", "pc2", "pc3", "pc4", "pc5", "pc7"], ["pc"], T.pc[:, 6:7], T.pc[:, 2:3], T.pc[:, 7:8], ALU.mult)
+    ts(["pc2", "pc7"], ["pc6"], T.pc[:, 6:7], T.pc[:, 2:3], T.pc[:, 7:8], ALU.mult)
     ts(["colf", "pc0", "wf"], ["BW"], T.BW[:], T.colf[:], T.pc[:, 0:1], ALU.is_equal, T.wf[:, 0:1], ALU.mult)
     ts(["colf"], ["ob"], T.ob[:], T.colf[:, 0:CD], 0.0, ALU.add)
-    ts(["colf", "pc"], ["onx"], T.onx[:], T.colf[:, 0:CD], 16.0, ALU.mult, T.pc[:, 6:7], ALU.add)
-    tt(["pA", "r2"], ["r3"], T.r3[:], T.pA[:, 0:C], T.r2[:], ALU.mult)
+    ts(["colf"], ["oc"], T.oc[:], T.colf[:, 0:HD], 2.0, ALU.mult, 1.0, ALU.add)
+    act(["pf"], ["ps4"], T.ps[:, 4:5], T.pf[:, 1:2], ACT.Identity, 17.0, 1.0)
+    ts(["colf", "pc3"], ["opa"], T.opa[:], T.colf[:, 0:CD], T.pc[:, 3:4], ALU.add)
+    ts(["colf", "pc6"], ["onx"], T.onx[:], T.colf[:, 0:CD], 16.0, ALU.mult, T.pc[:, 6:7], ALU.add)
     act(["colf", "ps2"], ["k1"], T.k1[:, 0:144], T.colf[:], ACT.Abs, T.ps[:, 2:3], 1.0)
     act(["colm", "ps0"], ["k2"], T.k2[:], T.colm[:], ACT.Abs, T.ps[:, 0:1], 1.0)
     act(["colf", "ps3"], ["k3"], T.k1[:, 144:152], T.colf[:, 0:8], ACT.Abs, T.ps[:, 3:4], 1.0)
@@ -248,195 +265,171 @@ def rank_program(g, core, T, topo):
     act(["rs1"], ["rsn"], T.rsn[:], T.rs1[:], ACT.Identity, 0.0, -1e20)
     act(["negI"], ["vI"], T.vI[:], T.negI[:], ACT.Identity, 0.0, BIG)
     act(["colm", "ps1"], ["m8"], T.m8[:], T.colm[:], ACT.Relu, T.ps[:, 1:2], 8192.0)
-    tt(["r3", "r1"], ["r4"], T.r4[:], T.r3[:], T.r1[:], ALU.add)
-    turn(T.r4[:], ["r4"], T.Rf[:, 0:C], "Rf")
-    cpv(["Rf"], ["mi0"], T.mi0[:, 0:C], T.Rf[:, 0:C])
-    ts(["colf"], ["oc"], T.oc[:], T.colf[:, 0:CD], float(CD), ALU.add)
-    ts(["colf", "pc"], ["opa"], T.opa[:], T.colf[:, 0:CD], T.pc[:, 3:4], ALU.add)
-    ts(["colf", "pc"], ["opb"], T.opb[:], T.colf[:, 0:CD], T.pc[:, 3:4], ALU.add, float(CD), ALU.add)
+    ts(["sgi"], ["sgb"], T.sgb[0:8, :], T.sgi[0:8, :], 0.0, ALU.is_lt)
+    cpv(["rli"], ["r1"], T.r1[:], T.rli[:])
+    mm(["E8T", "sgb"], ["pB"], T.pB[:, 0:C], T.E8T[0:8, :], T.sgb[0:8, :], True, True)
+    mm(["SH", "r1"], ["pA"], T.pA[:, 0:C], T.SH[:], T.r1[:], True, True, 4)
+    cps(["pB"], ["r2"], T.r2[:], T.pB[:, 0:C])
+    tt(["pA", "r2"], ["r3"], T.r3[:], T.pA[:, 0:C], T.r2[:], ALU.mult)
+    tt(["r3", "r1"], ["r2"], T.r2[:], T.r3[:], T.r1[:], ALU.add)
+    turn(T.r2[:], ["r2"], R, "Rf")
+    cpv(["Rf"], ["mi0"], T.mi0[:, 0:C], R)
 
-    def diagonal(name, src, B, bkey, out, okey, last):
-        def run(a, b, end):
-            for r in range(16):
-                mm(blocks(name, a, b) + [bkey], [okey], out[:, 16 * a:16 * b], B[:, 15 - r:143 - r],
-                   src[:, 256 * a + r:256 * b:16], False, end and r == 15)
-        return run
+    def probes(t, h):
+        c, b, pw, pk = slice(H * h, H * h + H), slice(HD * h, HD * h + HD), ("pW", "pB")[h], ("pK", "pA")[h]
+        i1, i2, u0, u1, dh, qi, qu, vo = [(x, h) for x in ("i1", "i2", "u0", "u1", "dh", "qi", "qu", "vo")]
+        Wh = T[pw][:, 0:H]
+        if t > 0:
+            tt([pw, "nb"], [i1], T.i1[:, c], Wh, T.nb[:, c], ALU.subtract)
+        else:
+            cpv([pw], [i1], T.i1[:, c], Wh)
+        ts([i1], [u0], T.u[:, b, 0:16], T.i1[:, c], W - 1, ALU.bitwise_and)
+        ts([i1], [u1], T.u[:, b, 16], T.i1[:, H * h:H * h + H:16], W - 1, ALU.bitwise_and)
+        tt([u0, u1], [i2], T.i2[:, c], T.u[:, b, 0:16], T.u[:, b, 1:17], ALU.mult)
+        ts([i2], [i1], T.i1[:, c], T.i2[:, c], 5, ALU.logical_shift_right)
+        tt([i1, pw], [i2], T.i2[:, c], Wh, T.i1[:, c], ALU.add)
+        ts([i2], [i1], T.i1[:, c], T.i2[:, c], 255, ALU.bitwise_and)
+        tt([i1, "pD0"], [dh], T.dh[:, c], T.pD[:, c], T.i1[:, c], ALU.mult)
+        tt([dh, "pD1"], [i2], T.i2[:, c], T.pD[:, C + H * h:C + H * h + H], T.dh[:, c], ALU.add)
+        ts([i2], [qi], T.qi[:, c], T.i2[:, c], W - 1, ALU.bitwise_and)
+        cpv([qi], [qu], T.qu[:, c], T.qi[:, c])
+        act([dh], [vo], T.vo[:, c], T.dh[:, c], ACT.Relu, 256.0, -256.0)
+        mm(["negI", "Rf"], [pk], T[pk][:, 0:H], T.negI[:], T.Rf[:, c], True, False, 4)
+        mm(["vI", vo], [pk], T[pk][:, 0:H], T.vI[:], T.vo[:, c], False, False)
 
-    def peers(t):
-        hop = HOP if t < TS - 1 else -HOP * t
-        return T.cores[(rank + hop) % N], T.cores[(rank - hop) % N]
+    def choose(t, h):
+        ai = "ai%d" % t
+        a, c, pk = HD * h, slice(H * h, H * h + H), ("pK", "pA")[h]
+        y, qi, run, nn = 3 * HD * h, ("qi", h), ("run", h), ("nn", h)
+        for cd in range(a, a + HD):
+            tt(["X", ("qu", h), ("Ab", cd)], [("D", cd)], T.D[:, 256 * cd:256 * cd + 256],
+               XT.indirect(T.qu[:, 16 * cd:16 * cd + 16]), T.Ab[:, cd, :], ALU.subtract, "gather")
+        for p, q in ABS_CH:
+            if a <= p < a + HD:
+                act(blocks("D", p, q), blocks("DA", p, q), T.DA[:, 256 * p:256 * q], T.D[:, 256 * p:256 * q], ACT.Abs, 0.0, 1.0)
+        diagonal("DA", "BE", pk, a, a + HD)
+        tt([qi, "DY"], [("DY0", h)], T.DY[:, H * h + 1:H * h + H], T.qi[:, H * h:H * h + H - 1], T.qi[:, H * h + 1:H * h + H],
+           ALU.subtract)
+        cpv([qi], [("Yl0", h)], T.Yl[:, y:y + HD], T.qi[:, H * h + 15:H * h + H:16])
+        cps(["Rf"], [("Yl1", h)], T.Yl[:, y + HD:y + 2 * HD], T.Rf[:, H * h:H * h + H:16])
+        cps(["Rf"], [("Yl2", h)], T.Yl[:, y + 2 * HD:y + 3 * HD], T.Rf[:, H * h + 15:H * h + H:16])
+        scan(["rsn", pk], [run], T.run[:, c], T.rsn[:, c], T[pk][:, 0:H], ALU.add, ALU.max)
+        tt([pk, run], [nn], T.nn[:, c], T[pk][:, 0:H], T.run[:, c], ALU.not_equal)
+        for j, k in enumerate((("DY0", h), "DY1", "DY2")):
+            scan([k, "DY", nn], [("wy", h, j)], T.wy[:, (3 * h + j) * H:(3 * h + j + 1) * H],
+                 T.DY[:, j * C + H * h:j * C + H * h + H], T.nn[:, c], ALU.add, ALU.mult)
+        for j in range(2):
+            cps([run], [("Kx", h, j)], T.Kx[:, j * CD + a:j * CD + a + HD], T.run[:, H * h + 15:H * h + H:16])
+        tt([("wy", h, j) for j in range(3)] + [("Yl%d" % j, h) for j in range(3)], [("Yb", h)], T.Yb[:, :, a:a + HD],
+           T.wy[:, 3 * H * h + 15:3 * H * (h + 1):16], T.Yl[:, y:y + 3 * HD], ALU.add)
+        cpv([("Yb", h)], [("o3", h)], T.o3[:, y:y + 3 * HD], T.Yb[:, :, a:a + HD])
+        for j in (1, 2, 0):
+            d = slice(j * C + H * h, j * C + H * h + H)
+            tt(["X", ("o3", h), ai], [("D3", j, h)], T.D3[:, d], XT.indirect(T.o3[:, y + j * HD:y + (j + 1) * HD]),
+               T[ai][:, c], ALU.subtract, "gather")
+            if j:
+                act([("D3", j, h)], [("T3", j, h)], T.T3[:, (j - 1) * C + H * h:(j - 1) * C + H * h + H], T.D3[:, d],
+                    ACT.Abs, 0.0, 1.0)
+        ts([("D3", 0, h)], [("T3", 0, h)], T.T3[:, 2 * C + H * h:2 * C + H * h + H], T.D3[:, c], 0.0, ALU.is_le)
 
-    def levels(t):
-        ai, mo, ao = "ai%d" % t, "mo%d" % t, "ao%d" % t
-
-        def second():
-            tt(["ta", ai], [ao], T[ao][:], T.ta[:], T[ai][:], ALU.add)
-            send(ao, "ai%d" % (t + 1), "ra%d" % (t + 1), peers(t)[0])
-            expect("ai%d" % (t + 1), "ra%d" % (t + 1), peers(t)[1])
-        return [lambda: tt(["w01", mo, "c3"], ["ta"], T.ta[:], T.w01[:].indirect(T[mo][:, C:C + CD]), T.c3[:], ALU.mult),
-                second]
-
-    R = T.Rf[:, 0:C]
-
-    def arrive(t):
-        mi = "mi%d" % t
-        return [lambda: cpv([mi], ["Rf"], T.Rf[:], T[mi][:]),
-                lambda: ts(["Rf"], ["pD"], T.pD[:, C:2 * C], R, -HALF, ALU.add),
-                lambda: cpv(["Rf", "onx"], ["Rn"], T.Rn[:], R.indirect(T.onx[:])),
-                lambda: tt(["Rn", "pD"], ["i3"], T.i3[:], T.Rn[:], T.pD[:, C:2 * C], ALU.subtract)]
-
-    def in_order():
-        calls = [lambda: cpv(["mi%d" % TS], ["sa0", "sa1"], T.sa[:], T["mi%d" % TS][:, 0:C])]
-        for a, b in (("sa", "sb"), ("sb", "sa")) * 2:
-            for j, o in ((0, ALU.min), (1, ALU.max)):
-                calls.append(lambda a=a, b=b, j=j, o=o: tt([a + "0", a + "1"], [b + str(j)], T[b][:, :, j:16:2],
-                                                           T[a][:, :, 0:8], T[a][:, :, 8:16], o))
-        return calls
-
-    for f in arrive(0)[1:]:
-        f()
-    rest, later = [], []
     for t in range(TS):
-        mi, ai, mo = "mi%d" % t, "ai%d" % t, "mo%d" % t
+        mi, ai, mo, ao = "mi%d" % t, "ai%d" % t, "mo%d" % t, "ao%d" % t
         M, A = T[mi], T[ai]
-        dst, src = peers(t)
 
-        def gather_r(e, a, b):
-            f = cpv if e == "V" else cps
-            f(["X", mi], blocks("G", a, b), T.G[:, 256 * a:256 * b], XT.indirect(M[:, 16 * a:16 * b]))
-        wsum = diagonal("G", T.G, T.BW, "BW", T.pW, "pW", True)
         if t > 0:
-            cps(["Rf", "ob"], ["gob"], T.gob[:], T.Rf[:, C:C + CD].indirect(T.ob[:]))
+            cpv([mi], ["Rf"], T.Rf[:], M[:])
+            cps(["Rf", "ob"], ["gob"], T.gob[:], T.Rf[:, C:C + CD].indirect(T.ob[:]), "gather")
             mm(["diag", "gob"], ["pN"], T.pN[:, 0:C], T.diag[:, 0:128], T.gob[:], True, True)
-            mm(["diag", "gob"], ["pW"], T.pW[:, 0:C], T.diag[:, 0:128], T.gob[:], True, False)
-        else:
-            mm(["zer"], ["pW"], T.pW[:, 0:C], T.zer[:, 0:128], T.zer[:], True, False)
-        for j in range(3):
-            gather_r("S", *R_S[j])
-            gather_r("V", *R_V[j])
-            wsum(PE_CH[j][0], PE_CH[j][1], j == 2)
-            if j == LATER:
-                for f in later:
-                    f()
-        for f in rest[FILL:]:
-            f()
-        mm(["negI", "Rf"], ["pK"], T.pK[:, 0:C], T.negI[:], R, True, False)
-        if t > 0:
             cps(["pN"], ["nb"], T.nb[:], T.pN[:, 0:C])
+        for h in range(2):
+            first = "gob" if t > 0 else "zer"
+            mm(["diag", first], [("pW", "pB")[h]], T[("pW", "pB")[h]][:, 0:H], T.diag[:, 0:128], T[first][:, H * h:H * h + H],
+               True, False)
+        ts(["Rf"], ["pD1"], T.pD[:, C:2 * C], R, -HALF, ALU.add)
+        cpv(["Rf", "onx"], ["Rn"], T.Rn[:], R.indirect(T.onx[:]), "gather")
+        tt(["Rn", "pD1"], ["i3"], T.i3[:], T.Rn[:], T.pD[:, C:2 * C], ALU.subtract)
         ts(["i3"], ["i4"], T.i4[:], T.i3[:], W - 1, ALU.bitwise_and)
-        ts(["i4"], ["pD"], T.pD[:, 0:C], T.i4[:], 1.0 / 256, ALU.mult)
-
-        for a, b in AB_CH:
-            cps([ai], [("Ab", a)], T.Ab[:, a:b, 0:16], A[:, 16 * a:16 * b])
-            for n in (16, 32, 64):
-                cps([("Ab", a)], [("Ab", a)], T.Ab[:, a:b, n:2 * n], T.Ab[:, a:b, 0:n])
-            cps([("Ab", a)], blocks("Ab", a, b), T.Ab[:, a:b, 128:256], T.Ab[:, a:b, 0:128])
-
-        if t > 0:
-            tt(["pW", "nb"], ["i1"], T.i1[:], T.pW[:, 0:C], T.nb[:], ALU.subtract)
-        else:
-            cpv(["pW"], ["i1"], T.i1[:], T.pW[:, 0:C])
-        ts(["i1"], ["u0"], T.u[:, :, 0:16], T.i1[:], W - 1, ALU.bitwise_and)
-        ts(["i1"], ["u1"], T.u[:, :, 16], T.i1[:, 0:C:16], W - 1, ALU.bitwise_and)
-        tt(["u0", "u1"], ["i2"], T.i2[:], T.u[:, :, 0:16], T.u[:, :, 1:17], ALU.mult)
-        ts(["i2"], ["i1"], T.i1[:], T.i2[:], 5, ALU.logical_shift_right)
-        tt(["i1", "pW"], ["i2"], T.i2[:], T.pW[:, 0:C], T.i1[:], ALU.add)
-        ts(["i2"], ["i1"], T.i1[:], T.i2[:], 255, ALU.bitwise_and)
-        tt(["i1", "pD"], ["dh"], T.dh[:], T.pD[:, 0:C], T.i1[:], ALU.mult)
-        tt(["dh", "pD"], ["i2"], T.i2[:], T.pD[:, C:2 * C], T.dh[:], ALU.add)
-        ts(["i2"], ["qi"], T.qi[:], T.i2[:], W - 1, ALU.bitwise_and)
-        cpv(["qi"], ["qu"], T.qu[:], T.qi[:])
-        op("S", ["dh"], ["vo"], lambda: g.scalar.activation(T.vo[:], T.dh[:], ACT.Relu, bias=256.0, scale=-256.0))
-        mm(["vI", "vo"], ["pK"], T.pK[:, 0:C], T.vI[:], T.vo[:], False, False)
-        cps(["Rf"], ["Yl1"], T.Yl[:, CD:2 * CD], T.Rf[:, 0:C:16])
-        cps(["Rf"], ["Yl2"], T.Yl[:, 2 * CD:3 * CD], T.Rf[:, 15:C:16])
-
-        esum = diagonal("DA", T.DA, T.BE, "BE", T.pK, "pK", True)
-        done = 0
-        for a, b in Q_CH:
-            for cd in range(a, b):
-                tt(["X", "qu", ("Ab", cd)], [("D", cd)], T.D[:, 256 * cd:256 * cd + 256],
-                   XT.indirect(T.qu[:, 16 * cd:16 * cd + 16]), T.Ab[:, cd, :], ALU.subtract)
-            op("S", blocks("D", a, b), blocks("DA", a, b),
-               lambda: g.scalar.activation(T.DA[:, 256 * a:256 * b], T.D[:, 256 * a:256 * b], ACT.Abs))
-            while done < len(PE_CH) and PE_CH[done][1] <= b:
-                esum(PE_CH[done][0], PE_CH[done][1], done == len(PE_CH) - 1)
-                done += 1
-        tt(["qi", "DY"], ["DY0"], T.DY[:, 1:C], T.qi[:, 0:C - 1], T.qi[:, 1:C], ALU.subtract)
+        ts(["i4"], ["pD0"], T.pD[:, 0:C], T.i4[:], 1.0 / 256, ALU.mult)
         tt(["Rf", "Rn", "DY"], ["DY1"], T.DY[:, C + 1:2 * C:2], T.Rf[:, 0:C:2], T.Rn[:, 1:C:2], ALU.subtract)
         tt(["Rf", "Rn", "DY"], ["DY2"], T.DY[:, 2 * C + 2:3 * C:2], T.Rf[:, 1:C - 1:2], T.Rn[:, 2:C:2], ALU.subtract)
-        cpv(["qi"], ["Yl0"], T.Yl[:, 0:CD], T.qi[:, 15:C:16])
-        scan(["rsn", "pK"], ["run"], T.run[:], T.rsn[:], T.pK[:, 0:C], ALU.add, ALU.max)
-        tt(["pK", "run"], ["nn"], T.nn[:], T.pK[:, 0:C], T.run[:], ALU.not_equal)
-        for j in range(3):
-            scan(["DY%d" % j, "DY", "nn"], ["wy%d" % j], T.wy[:, j * C:(j + 1) * C], T.DY[:, j * C:(j + 1) * C], T.nn[:],
-                 ALU.add, ALU.mult)
-        cps(["run"], ["Kx0"], T.Kx[:, 0:CD], T.run[:, 15:C:16])
-        cps(["run"], ["Kx1"], T.Kx[:, CD:2 * CD], T.run[:, 15:C:16])
-        tt(["wy0", "wy1", "wy2", "Yl0", "Yl1", "Yl2"], ["Yb"], T.Yb[:], T.wy[:, 15:3 * C:16], T.Yl[:], ALU.add)
-        cpv(["Yb"], ["o3"], T.o3[:], T.Yb[:])
 
-        for j in (1, 2, 0):
-            tt(["X", "o3", ai], [("D3", j)], T.D3[:, j * C:(j + 1) * C], XT.indirect(T.o3[:, j * CD:(j + 1) * CD]), A[:],
-               ALU.subtract)
-            if j:
-                op("S", [("D3", j)], [("T3", j)],
-                   lambda: g.scalar.activation(T.T3[:, (j - 1) * C:j * C], T.D3[:, j * C:(j + 1) * C], ACT.Abs))
-        ts([("D3", 0)], [("T3", 0)], T.T3[:, 2 * C:3 * C], T.D3[:, 0:C], 0.0, ALU.is_le)
+        for e, a, b in R_CH:
+            (cpv if e == "V" else cps)(["X", mi], blocks("G", a, b), T.G[:, 256 * a:256 * b],
+                                       XT.indirect(M[:, 16 * a:16 * b]), "gather")
+            behind(*[("G", x) for y, x, z in R_CH if x < a])
+        for h in range(2):
+            a, b = HD * h, HD * h + HD
+            diagonal("G", "BW", ("pW", "pB")[h], a, b)
+            cps([ai], blocks("Ab", a, b), T.Ab[:, a:b, 0:16], A[:, 16 * a:16 * b])
+            behind(("G", CD - 1), ("G", HD - 1))
+            for n in (16, 32, 64, 128):
+                cps(blocks("Ab", a, b), blocks("Ab", a, b), T.Ab[:, a:b, n:2 * n], T.Ab[:, a:b, 0:n])
+        for h in range(2):
+            probes(t, h)
+        for h in range(2):
+            choose(t, h)
+
+        Yb = [("Yb", 0), ("Yb", 1)]
         for r in range(16):
-            mm(blocks("T3", 0, 3) + ["BE"], ["p3"], T.p3[:, 0:3 * CD], T.BE[:, 15 - r:143 - r], T.T3[:, r:3 * C:16],
-               r == 0, r == 15)
-        tt(["Yb", "opb", "Rf"], ["mm"], T.mm[:], T.Yb[:].indirect(T.opb[:]), R, ALU.is_equal)
-        tt(["Yb"], ["dl0"], T.dl[:, 0:CD], T.Yb[:, 0:CD], T.Yb[:, CD:2 * CD], ALU.subtract)
-        tt(["Yb"], ["dl1"], T.dl[:, CD:2 * CD], T.Yb[:, 0:CD], T.Yb[:, 2 * CD:3 * CD], ALU.subtract)
-        ts(["Yb"], ["ee"], T.ee[:], T.Yb[:, CD:3 * CD], float(PAD), ALU.add)
-        ts([("D3", 0)], ["c3"], T.c3[:], T.D3[:, 0:C], -3.0, ALU.max, 3.0, ALU.min)
-        tt(["p3", "Kx0", "Kx1", "Kx2"], ["F"], T.F[:], T.p3[:, 0:3 * CD], T.Kx[:], ALU.is_lt)
+            mm([("T3", j, h) for j in range(3) for h in range(2)] + ["BE"], ["p3"], T.p3[:, 0:3 * CD],
+               T.BE[:, 15 - r:143 - r], T.T3[:, r:3 * C:16], r == 0, r == 15)
+        cps(Yb, ["rp"], T.rp[:], T.Yb[:, 1:3, :])
+        act(Yb, ["ee"], T.ee[:], T.Yb[:, 1:3, :], ACT.Identity, float(PAD), 1.0)
+        tt(["rp", "opa", "Rf"], ["mm"], T.mm[:], T.rp[:].indirect(T.opa[:]), R, ALU.is_equal, "gather")
+        tt(Yb, ["dl0"], T.dl[:, 0:CD], T.Yb[:, 0, :], T.Yb[:, 1, :], ALU.subtract)
+        tt(Yb, ["dl1"], T.dl[:, CD:2 * CD], T.Yb[:, 0, :], T.Yb[:, 2, :], ALU.subtract)
+        ts([("D3", 0, 0), ("D3", 0, 1)], ["c3"], T.c3[:], T.D3[:, 0:C], -3.0, ALU.max, 3.0, ALU.min)
+        tt(["p3", "Kx2"] + [("Kx", h, j) for h in range(2) for j in range(2)], ["F"], T.F[:], T.p3[:, 0:3 * CD], T.Kx[:],
+           ALU.is_lt)
         tt(["F"], ["gg0"], T.gg[:, 0:CD], T.F[:, 0:CD], T.F[:, 2 * CD:3 * CD], ALU.mult)
         tt(["F"], ["gg1"], T.gg[:, CD:2 * CD], T.F[:, CD:2 * CD], T.F[:, 2 * CD:3 * CD], ALU.is_gt)
-        tt(["gg0", "gg1", "dl0", "dl1"], ["dg"], T.dg[:], T.gg[:], T.dl[:], ALU.mult)
-        KA, KU = T.MF[:, C + CD:C + 2 * CD], T[mo][:, C + CD:C + 2 * CD]
+        KA, KU = T.ka[:, 0:CD], T.ku[:, 0:CD]
+        tt(["dl0", "dl1", "opa", "mm"], ["cand"], T.cand[:], T.dl[:].indirect(T.opa[:]), T.mm[:], ALU.mult, "gather")
         tt(["gg0", "gg1", "ee"], ["te"], T.te[:], T.gg[:], T.ee[:], ALU.mult)
-        tt(["dg", "opa", "mm"], ["rr"], T.rr[:], T.dg[:].indirect(T.opa[:]), T.mm[:], ALU.mult)
+        tt(["gg0", "gg1", "opa", "cand"], ["rr"], T.rr[:], T.gg[:].indirect(T.opa[:]), T.cand[:], ALU.mult, "gather")
         tt(["gg0", "gg1"], ["MF1"], T.MF[:, C:C + CD], T.gg[:, 0:CD], T.gg[:, CD:2 * CD], ALU.add)
         tt(["te"], ["ka"], KA, T.te[:, 0:CD], T.te[:, CD:2 * CD], ALU.add)
-        tt(["rr", "pD"], ["MF0"], T.MF[:, 0:C], T.pD[:, C:2 * C], T.rr[:], ALU.add)
-        ts(["MF0", "MF1", "ka"], [mo], T[mo][:], T.MF[:], HALF, ALU.add)
-        send(mo, "mi%d" % (t + 1), "rm%d" % (t + 1), dst)
-        expect("mi%d" % (t + 1), "rm%d" % (t + 1), src)
-        rest = arrive(t + 1) if t < TS - 1 else in_order()
-        now, later = (levels(t), []) if LATER < 0 or t == TS - 1 else ([None, None], levels(t))
-        fill = now + [None] * (CD - 2 - FILL) + rest[:FILL]
+        tt(["te"], ["ke"], T.ka[:, CD:CD + HD], T.te[:, 0:CD:2], T.te[:, CD:2 * CD:2], ALU.add)
+        cpv(["ka", "ke"], ["ku"], T.ku[:], T.ka[:])
+        tt(["rr", "pD1"], ["MF0"], T.MF[:, 0:C], T.pD[:, C:2 * C], T.rr[:], ALU.add)
+        ts(["MF0", "MF1"], [mo], T[mo][:], T.MF[:], HALF, ALU.add)
+        send(mo, "mi%d" % (t + 1), "rm%d" % (t + 1), t)
 
-        tt(["IOT", mo, "m8"], ["Nm"], T.Nm[:], T.IOT[:].indirect(KU), T.m8[:], ALU.add)
-        act(["X", "Xpad", mo], ["xl"], T.xl[:], T.X[:].indirect(KU), ACT.Identity, -5.0, 1.0)
-        tt(["X", "Xpad", mo, ai], ["dx"], T.dx[:], T.X[:].indirect(KU), A[:], ALU.subtract)
+        tt(["w01", mo, "c3"], ["ta"], T.ta[:], T.w01[:].indirect(T[mo][:, C:C + CD]), T.c3[:], ALU.mult, "gather")
+        tt(["ta", ai], [ao], T[ao][:], T.ta[:], A[:], ALU.add)
+        send(ao, "ai%d" % (t + 1), "ra%d" % (t + 1), t)
+
+        tt(["IOT", "ku", "m8"], ["Nm"], T.Nm[:], T.IOT[:].indirect(KU), T.m8[:], ALU.add, "gather")
+        cps(["IOT", "ku"], ["Ne"], T.Ne[:], T.IOT[:].indirect(T.ku[:, CD:CD + HD]), "gather")
+        act(["X", "Xpad", "ku"], ["xl"], T.xl[:], T.X[:].indirect(KU), ACT.Identity, -5.0, 1.0, "gather")
+        tt(["X", "Xpad", "ku", ai], ["dx"], T.dx[:], T.X[:].indirect(KU), A[:], ALU.subtract, "gather")
         act(["dx"], ["c4"], T.c4[:], T.dx[:], ACT.Relu, 5.0, 1.0)
         act(["c4"], ["c5"], T.c5[:], T.c4[:], ACT.Relu, 10.0, -1.0)
-        tt(["ka", "MF1", "oc", "Nm"], ["ne"], T.ne[:], T.MF[:, C:C + 2 * CD].indirect(T.oc[:]), T.Nm[:], ALU.not_equal)
+        tt(["ka", "ke", "ob", "Nm"], ["ne"], T.ne[:], T.ka[:].indirect(T.ob[:]), T.Nm[:], ALU.not_equal, "gather")
+        tt(["ka", "ke", "oc", "Ne"], ["n2"], T.n2[:], T.ka[:].indirect(T.oc[:]), T.Ne[:], ALU.not_equal, "gather")
         scan(["rs1", "ne"], ["nd"], T.nd[:], T.rs1[:], T.ne[:], ALU.max, ALU.min)
-        tt(["ka", "nd"], ["kn"], T.kn[:], KA, T.nd[:, 15:C:16], ALU.mult)
-        if fill[0] is not None:
-            fill[0]()
-        ts(["kn", "pc"], ["lo"], T.lo[:, 0:2 * CD:2], T.kn[:], T.pc[:, 2:3], ALU.max)
-        for cd in range(CD - 1, -1, -1):
-            tt(["lo", "xl", "c5"], ["X", "Xpad"], T.X[:].indirect(T.lo[:, 2 * cd:2 * cd + 1]),
-               T.xl[:, 16 * cd:16 * cd + 16], T.c5[:, 16 * cd:16 * cd + 16], ALU.add)
-            if cd > 0 and fill[CD - cd] is not None:
-                fill[CD - cd]()
+        scan(["rs1", "n2"], ["n3"], T.n3[:], T.rs1[:, 0:H], T.n2[:], ALU.max, ALU.min)
+        cps(["ka"], ["kb0"], T.kb[:, 0:CD:2], T.ka[:, 0:CD:2])
+        tt(["ka", "n3"], ["kb1"], T.kb[:, 1:CD:2], T.ka[:, 1:CD:2], T.n3[:, 15:H:16], ALU.mult)
+        tt(["kb0", "kb1", "nd"], ["kn"], T.kn[:], T.kb[:], T.nd[:, 15:C:16], ALU.mult)
+        ts(["kn", "pc2"], ["lo0"], T.lo[:, 0:CD:2], T.kn[:, 0:CD:2], T.pc[:, 2:3], ALU.max)
+        ts(["kn", "ps4"], ["lo1"], T.lo[:, 1:CD:2], T.kn[:, 1:CD:2], T.ps[:, 4:5], ALU.max)
+        for cd in range(CD - 2, -1, -2):
+            tt(["lo0", "lo1", "xl", "c5"], ["X", "Xpad"], T.X[:].indirect(T.lo[:, cd:cd + 2]),
+               T.xl[:, 16 * cd:16 * cd + 32], T.c5[:, 16 * cd:16 * cd + 32], ALU.add, "scatter")
 
-    dma("Y", "ox", ["X"], [], T.yx[:], XT)
     mi, ai = "mi%d" % TS, "ai%d" % TS
+    dma("Y", "ox", ["X"], [], T.yx[:], XT)
     dma("S", "oa", [ai], [], T.ya[:], T[ai][:])
-    for f in rest[FILL:]:
-        f()
-    a, b = "sa", "sb"
-    turn(T[a][:], [a + "0", a + "1"], T.r1[:], "r1")
+    cpv([mi], ["sa0", "sa1"], T.sa[:], T[mi][:, 0:C])
+    for a, b in (("sa", "sb"), ("sb", "sa")) * 2:
+        for j, o in ((0, ALU.min), (1, ALU.max)):
+            tt([a + "0", a + "1"], [b + str(j)], T[b][:, :, j:16:2], T[a][:, :, 0:8], T[a][:, :, 8:16], o)
+    turn(T.sa[:], ["sa0", "sa1"], T.r1[:], "r1")
     dma("Y", "orr", ["r1"], [], T.yr[:], T.r1[:])
-    tt([b + "0", b + "1"], ["sf"], T.sf[:, 0:CD], T[b][:, :, 0], T[b][:, :, 8], ALU.is_lt)
-    tt(["sf", "ob", "diag"], ["sx"], T.sx[:], T.sf[:].indirect(T.ob[:]), T.diag[:], ALU.mult)
+    tt(["sb0", "sb1"], ["sf"], T.sf[:, 0:CD], T.sb[:, :, 0], T.sb[:, :, 8], ALU.is_lt)
+    tt(["sf", "ob", "diag"], ["sx"], T.sx[:], T.sf[:].indirect(T.ob[:]), T.diag[:], ALU.mult, "gather")
     mm(["E8", "sx"], ["pA"], T.pA[0:8, 0:C], T.E8[:], T.sx[:], True, True)
     act(["pA"], ["so"], T.so[0:8, :], T.pA[0:8, 0:C], ACT.Identity, -1.0, 2.0)
     dma("S", "osg", ["so"], [], T.ys[:], T.so[0:8, :])
-    for s, v in final.items():
-        wait("G", s, v)
+    emit()

@@ -16,28 +16,31 @@ SCRATCH = {"Ab": ("sbuf", [128, CD, 256], BF), "u": ("sbuf", [128, CD, 17], I32)
 for _names, _n, _d in (
         ("X", W + PAD, BF), ("IOT", W + PAD, F32), ("G D DA", 16 * C, BF),
         ("ti", 8, I32), ("pf pc", 8, F32), ("ps", 5, F32), ("oc", HD, U16), ("Ne n2 n3", H, F32), ("cand", C, F32),
-        ("ka", CD + HD, F32), ("ku", CD + HD, U16), ("kb", CD, F32), ("wi", 1, I32), ("wf", 1, F32),
+        ("ka", CD + HD, F32), ("ku", CD + HD, U16), ("kb", CD, F32), ("wi", 1, I32),
         ("cp chi negI SH pm1", 128, F32), ("vI E8T", 128, BF), ("colf", 144, F32), ("k1", 152, F32), ("BW BE", 144, BF),
         ("E8", 8, BF), ("w01", 16, BF), ("sf", 16, F32), ("ob opa onx lo", CD, U16),
-        ("colm k2 m8 rsn rs1 r1 r2 r3 so Rn nb dh run nn mm rr Nm ne nd", C, F32),
+        ("colm m8 rsn rs1 r1 r2 r3 so Rn nb dh run nn mm rr Nm ne nd", C, F32),
         ("diag zer sgb sx gob vo c3 ta xl dx c4 c5", C, BF), ("rli sgi i1 i2 i3 i4 qi", C, I32), ("qu", C, U16),
         ("Rf MF", C + CD, F32), ("DY wy", 3 * C, F32), ("D3 T3", 3 * C, BF),
-        ("Yl Kx F", 3 * CD, F32), ("o3", 3 * CD, U16), ("gg dl ee te rp", 2 * CD, F32), ("kn", CD, F32),
+        ("Yl", 3 * CD, F32), ("o3", 3 * CD, U16), ("gg dl ee te rp Kx Ky F", 2 * CD, F32), ("kn", CD, F32),
         ("mi0 mi1 mi2 mi3 mi4 mi5", C + CD, U16),
         ("mo0 mo1 mo2 mo3 mo4", C + CD, U16),
         ("ai0 ai1 ai2 ai3 ai4 ai5 ao0 ao1 ao2 ao3 ao4", C, BF)):
     for _x in _names.split():
         SCRATCH[_x] = ("sbuf", [128, _n], _d)
 PSUM = ("pW", "pK", "p3", "pN", "pA", "pB")
-for _x in PSUM + ("pD",):
+for _x in PSUM + ("pD", "pR"):
     SCRATCH[_x] = ("psum", [128, 512], F32)
 
 SEMAPHORES = (["cV", "cS", "cP", "cG", "sent", "lx", "lr", "la", "ls", "lw", "ox", "oa", "orr", "osg"]
               + ["rm%d" % t for t in range(1, TS + 1)] + ["ra%d" % t for t in range(1, TS + 1)])
 
 R_CH = [("V", 0, 3), ("S", 3, 6), ("V", 6, 8), ("S", 8, 12)]
+OPT = [1, 0, 0]
+PARTS = [(0, 8), (8, 12)]
 ABS_CH = [(0, 2), (2, 4), (4, 6), (6, 8), (8, 10), (10, 11), (11, 12)]
-CYCLE, PE_CYCLE, WAKE, SLACK, FLIGHT = 0.9, 0.8, 140.0, 20.0, 3500.0
+CYCLE, PE_CYCLE, WAKE, SLACK, FLIGHT = 0.9, 0.6, 160.0, 20.0, 3500.0
+SPREAD, SALT = 0.0, 1
 
 
 def rank_program(g, core, T, topo):
@@ -87,6 +90,8 @@ def rank_program(g, core, T, topo):
         tail = [0.0] * n
         for i in range(n - 1, -1, -1):
             tail[i] = ops[i]["cost"] + max([gap(i, j) + tail[j] for j in after[i]] + [ops[i]["lat"]])
+        for i in range(n):
+            tail[i] += SPREAD * ((i * SALT) % 1009) / 1009.0
         left = [len(o["deps"]) for o in ops]
         ready_at = [0.0] * n
         ready = [i for i in range(n) if left[i] == 0]
@@ -141,7 +146,7 @@ def rank_program(g, core, T, topo):
             if slow:
                 return Q[e].dma_start(out, in_, allow_slow_non_contiguous=True)
             return Q[e].dma_start(out, in_)
-        add(e, reads, writes, call, 100.0, 2000.0 + 1.3 * size(out), sem, 16)
+        add(e, reads, writes, call, 100.0, 2000.0 + 0.6 * size(out), sem, 16)
 
     def lanes(src, dst):
         m = 0
@@ -176,6 +181,9 @@ def rank_program(g, core, T, topo):
     def cps(r, w, out, a, kind=None):
         add("S", r, w, lambda: g.scalar.activation(out, a, ACT.Copy), price(out, 1, kind))
 
+    def cpg(r, w, out, a):
+        add("G", r, w, lambda: g.affine_select(out, a, [[0, size(out)]], ALU.is_gt, 0.0, 1, 0), 170.0 + 2 * size(out) * CYCLE)
+
     def act(r, w, out, a, func, bias, scale, kind=None):
         add("S", r, w, lambda: g.scalar.activation(out, a, func, bias=bias, scale=scale), price(out, 1, kind))
 
@@ -195,15 +203,17 @@ def rank_program(g, core, T, topo):
     def blocks(name, a, b):
         return [(name, i) for i in range(a, b)]
 
-    def turn(src, src_keys, dst, dst_key):
-        ts(src_keys + ["pc4"], ["Z0"], T.Z[:, :, 0:16], src, T.pc[:, 4:5], ALU.mult)
-        ts(src_keys + ["pf"], ["Z1"], T.Z[:, :, 16:32], src, T.pf[:, 3:4], ALU.mult)
-        add("V", ["Z0", "Z1"], ["Zt"], lambda: g.vector.transpose(T.Zt[:], T.Z[:]), price(T.Zt[:], 1))
-        tt(["Zt"], [dst_key], dst, T.Zt[:, :, 0:16], T.Zt[:, :, 16:32], ALU.add)
+    def turn(src, src_keys, dst, dst_key, h):
+        s = slice(HD * h, HD * h + HD)
+        ts(src_keys + ["pc4"], [("Z0", h)], T.Z[:, s, 0:16], src, T.pc[:, 4:5], ALU.mult)
+        act(src_keys + ["pf"], [("Z1", h)], T.Z[:, s, 16:32], src, ACT.Identity, 0.0, T.pf[:, 3:4])
+        add("V", [("Z0", h), ("Z1", h)], [("Zt", h)], lambda: g.vector.transpose(T.Zt[:, s, :], T.Z[:, s, :]),
+            price(T.Zt[:, s, :], 1))
+        tt([("Zt", h)], [dst_key], dst, T.Zt[:, s, 0:16], T.Zt[:, s, 16:32], ALU.add)
 
     def diagonal(name, B, out, a, b):
         for r in range(16):
-            mm(blocks(name, a, b) + [B], [out], T[out][:, 0:16 * (b - a)], T[B][:, 15 - r:143 - r],
+            mm(blocks(name, a, b) + [B], [out, "order " + B], T[out][:, 0:16 * (b - a)], T[B][:, 15 - r:143 - r],
                T[name][:, 256 * a + r:256 * b:16], False, r == 15)
 
     XT = T.X[:, PAD:PAD + W]
@@ -212,15 +222,14 @@ def rank_program(g, core, T, topo):
     dma("S", "lr", [], ["rli"], T.rli[:], T.rl[:])
     dma("Y", "ls", [], ["sgi"], T.sgi[0:8, :], T.sg[:])
     dma("Y", "lx", [], ["X"], XT, T.xt[:])
-    dma("S", "la", ["pf"], ["ai0"], T.ai0[:], T.av[:])
-    dma("G", "lw", ["cp"], ["wi"], T.wi[:], T.wt[:], slow=True)
+    dma("S", "la", [], ["ai0"], T.ai0[:], T.av[:])
+    dma("G", "lw", [], ["wi"], T.wi[:], T.wt[:], slow=True)
     add("G", [], ["ti0"], lambda: g.iota(T.ti[:, 0:1], [[0, 1]], 0, 1), 130.0)
     iota(["colf"], T.colf[:], [[1, 144]], 0, 0)
     iota(["cp"], T.cp[:], [[1, 128]], 0, -1)
     iota(["chi"], T.chi[0:8, :], [[1, 8], [0, 16]], 0, -1)
     iota(["colm"], T.colm[:], [[0, CD], [1, 16]], 0, 0)
     iota(["DY"], T.DY[:], [[0, 3 * C]], 0, 0)
-    iota(["Kx2"], T.Kx[:, 2 * CD:3 * CD], [[0, CD]], 17 * 2048, 0)
     iota(["w01"], T.w01[:], [[1, 16]], 0, 0)
     iota(["sf"], T.sf[:], [[0, 16]], 0, 0)
     iota(["IOT"], T.IOT[:], [[1, W + PAD]], 0, 0)
@@ -247,20 +256,20 @@ def rank_program(g, core, T, topo):
     act(["pf"], ["ps3"], T.ps[:, 3:4], T.pf[:, 2:3], ACT.Identity, 0.0, -1.0)
     tt(["pm1", "negI"], ["SH"], T.SH[:], T.pm1[:], T.negI[:], ALU.add)
     ts(["pf"], ["pc7"], T.pc[:, 7:8], T.pf[:, 1:2], 15.0, ALU.is_lt)
-    cpv(["wi"], ["wf"], T.wf[:], T.wi[:])
+    cpv(["wi"], ["wf"], T.pf[:, 5:6], T.wi[:])
     ts(["pc2", "pc7"], ["pc6"], T.pc[:, 6:7], T.pc[:, 2:3], T.pc[:, 7:8], ALU.mult)
-    ts(["colf", "pc0", "wf"], ["BW"], T.BW[:], T.colf[:], T.pc[:, 0:1], ALU.is_equal, T.wf[:, 0:1], ALU.mult)
+    ts(["colf", "pc0", "wf"], ["BW"], T.BW[:], T.colf[:], T.pc[:, 0:1], ALU.is_equal, T.pf[:, 5:6], ALU.mult)
     ts(["colf"], ["ob"], T.ob[:], T.colf[:, 0:CD], 0.0, ALU.add)
     ts(["colf"], ["oc"], T.oc[:], T.colf[:, 0:HD], 2.0, ALU.mult, 1.0, ALU.add)
     act(["pf"], ["ps4"], T.ps[:, 4:5], T.pf[:, 1:2], ACT.Identity, 17.0, 1.0)
     ts(["colf", "pc3"], ["opa"], T.opa[:], T.colf[:, 0:CD], T.pc[:, 3:4], ALU.add)
     ts(["colf", "pc6"], ["onx"], T.onx[:], T.colf[:, 0:CD], 16.0, ALU.mult, T.pc[:, 6:7], ALU.add)
     act(["colf", "ps2"], ["k1"], T.k1[:, 0:144], T.colf[:], ACT.Abs, T.ps[:, 2:3], 1.0)
-    act(["colm", "ps0"], ["k2"], T.k2[:], T.colm[:], ACT.Abs, T.ps[:, 0:1], 1.0)
+    act(["colm", "ps0"], ["Nm"], T.Nm[:], T.colm[:], ACT.Abs, T.ps[:, 0:1], 1.0)
     act(["colf", "ps3"], ["k3"], T.k1[:, 144:152], T.colf[:, 0:8], ACT.Abs, T.ps[:, 3:4], 1.0)
     act(["colm"], ["rs1"], T.rs1[:], T.colm[:], ACT.Relu, 1.0, -1.0)
     act(["k1"], ["BE"], T.BE[:], T.k1[:, 0:144], ACT.Relu, 4096.0, -4096.0)
-    act(["k2"], ["diag"], T.diag[:], T.k2[:], ACT.Relu, 1.0, -1.0)
+    act(["Nm"], ["diag"], T.diag[:], T.Nm[:], ACT.Relu, 1.0, -1.0)
     act(["k3"], ["E8"], T.E8[:], T.k1[:, 144:152], ACT.Relu, 1.0, -1.0)
     act(["rs1"], ["rsn"], T.rsn[:], T.rs1[:], ACT.Identity, 0.0, -1e20)
     act(["negI"], ["vI"], T.vI[:], T.negI[:], ACT.Identity, 0.0, BIG)
@@ -270,10 +279,13 @@ def rank_program(g, core, T, topo):
     mm(["E8T", "sgb"], ["pB"], T.pB[:, 0:C], T.E8T[0:8, :], T.sgb[0:8, :], True, True)
     mm(["SH", "r1"], ["pA"], T.pA[:, 0:C], T.SH[:], T.r1[:], True, True, 4)
     cps(["pB"], ["r2"], T.r2[:], T.pB[:, 0:C])
-    tt(["pA", "r2"], ["r3"], T.r3[:], T.pA[:, 0:C], T.r2[:], ALU.mult)
-    tt(["r3", "r1"], ["r2"], T.r2[:], T.r3[:], T.r1[:], ALU.add)
-    turn(T.r2[:], ["r2"], R, "Rf")
-    cpv(["Rf"], ["mi0"], T.mi0[:, 0:C], R)
+    for h in range(2):
+        c = slice(H * h, H * h + H)
+        tt(["pA", "r2"], [("r3", h)], T.r3[:, c], T.pA[:, c], T.r2[:, c], ALU.mult)
+        tt([("r3", h), "r1"], [("so", h)], T.so[:, c], T.r3[:, c], T.r1[:, c], ALU.add)
+        turn(T.so[:, c], [("so", h)], T.r3[:, c], ("r3", h), h)
+    cpv(blocks("r3", 0, 2), ["mi0"], T.mi0[:, 0:C], T.r3[:])
+    cps(blocks("r3", 0, 2), ["Rf"], R, T.r3[:])
 
     def probes(t, h):
         c, b, pw, pk = slice(H * h, H * h + H), slice(HD * h, HD * h + HD), ("pW", "pB")[h], ("pK", "pA")[h]
@@ -290,47 +302,50 @@ def rank_program(g, core, T, topo):
         tt([i1, pw], [i2], T.i2[:, c], Wh, T.i1[:, c], ALU.add)
         ts([i2], [i1], T.i1[:, c], T.i2[:, c], 255, ALU.bitwise_and)
         tt([i1, "pD0"], [dh], T.dh[:, c], T.pD[:, c], T.i1[:, c], ALU.mult)
-        tt([dh, "pD1"], [i2], T.i2[:, c], T.pD[:, C + H * h:C + H * h + H], T.dh[:, c], ALU.add)
+        tt([dh, "pD1"], [i2], T.i2[:, c], T.pR[:, c], T.dh[:, c], ALU.add)
         ts([i2], [qi], T.qi[:, c], T.i2[:, c], W - 1, ALU.bitwise_and)
         cpv([qi], [qu], T.qu[:, c], T.qi[:, c])
         act([dh], [vo], T.vo[:, c], T.dh[:, c], ACT.Relu, 256.0, -256.0)
-        mm(["negI", "Rf"], [pk], T[pk][:, 0:H], T.negI[:], T.Rf[:, c], True, False, 4)
-        mm(["vI", vo], [pk], T[pk][:, 0:H], T.vI[:], T.vo[:, c], False, False)
 
     def choose(t, h):
         ai = "ai%d" % t
-        a, c, pk = HD * h, slice(H * h, H * h + H), ("pK", "pA")[h]
-        y, qi, run, nn = 3 * HD * h, ("qi", h), ("run", h), ("nn", h)
-        for cd in range(a, a + HD):
-            tt(["X", ("qu", h), ("Ab", cd)], [("D", cd)], T.D[:, 256 * cd:256 * cd + 256],
+        a, b = PARTS[h]
+        n, p, q, pk = b - a, 16 * a, 16 * b, ("pK", "pA")[h]
+        c, key = slice(p, q), T[pk][:, 0:16 * n]
+        y, qi, run, nn = 3 * a, blocks("qi", 0, 2), ("run", h), ("nn", h)
+        mm(["negI", "Rf"], [pk], key, T.negI[:], T.Rf[:, c], True, False, 4)
+        mm(["vI"] + blocks("vo", 0, 2), [pk], key, T.vI[:], T.vo[:, c], False, False)
+        for cd in range(a, b):
+            tt(["X", ("qu", cd // HD), ("Ab", cd)], [("D", cd)], T.D[:, 256 * cd:256 * cd + 256],
                XT.indirect(T.qu[:, 16 * cd:16 * cd + 16]), T.Ab[:, cd, :], ALU.subtract, "gather")
-        for p, q in ABS_CH:
-            if a <= p < a + HD:
-                act(blocks("D", p, q), blocks("DA", p, q), T.DA[:, 256 * p:256 * q], T.D[:, 256 * p:256 * q], ACT.Abs, 0.0, 1.0)
-        diagonal("DA", "BE", pk, a, a + HD)
-        tt([qi, "DY"], [("DY0", h)], T.DY[:, H * h + 1:H * h + H], T.qi[:, H * h:H * h + H - 1], T.qi[:, H * h + 1:H * h + H],
-           ALU.subtract)
-        cpv([qi], [("Yl0", h)], T.Yl[:, y:y + HD], T.qi[:, H * h + 15:H * h + H:16])
-        cps(["Rf"], [("Yl1", h)], T.Yl[:, y + HD:y + 2 * HD], T.Rf[:, H * h:H * h + H:16])
-        cps(["Rf"], [("Yl2", h)], T.Yl[:, y + 2 * HD:y + 3 * HD], T.Rf[:, H * h + 15:H * h + H:16])
-        scan(["rsn", pk], [run], T.run[:, c], T.rsn[:, c], T[pk][:, 0:H], ALU.add, ALU.max)
-        tt([pk, run], [nn], T.nn[:, c], T[pk][:, 0:H], T.run[:, c], ALU.not_equal)
-        for j, k in enumerate((("DY0", h), "DY1", "DY2")):
-            scan([k, "DY", nn], [("wy", h, j)], T.wy[:, (3 * h + j) * H:(3 * h + j + 1) * H],
-                 T.DY[:, j * C + H * h:j * C + H * h + H], T.nn[:, c], ALU.add, ALU.mult)
+            if OPT[2]:
+                behind(("D", cd - 1))
+        for r, s in ABS_CH:
+            if a <= r < b:
+                act(blocks("D", r, s), blocks("DA", r, s), T.DA[:, 256 * r:256 * s], T.D[:, 256 * r:256 * s], ACT.Abs, 0.0, 1.0)
+        diagonal("DA", "BE", pk, a, b)
+        if h == 0:
+            tt(qi + ["DY"], ["DY0"], T.DY[:, 1:C], T.qi[:, 0:C - 1], T.qi[:, 1:C], ALU.subtract)
+        cpv(qi, [("Yl0", h)], T.Yl[:, y:y + n], T.qi[:, p + 15:q:16])
+        cps(["Rf"], [("Yl1", h)], T.Yl[:, y + n:y + 2 * n], T.Rf[:, p:q:16])
+        cps(["Rf"], [("Yl2", h)], T.Yl[:, y + 2 * n:y + 3 * n], T.Rf[:, p + 15:q:16])
+        scan(["rsn", pk], [run], T.run[:, c], T.rsn[:, c], key, ALU.add, ALU.max)
+        tt([pk, run], [nn], T.nn[:, c], key, T.run[:, c], ALU.not_equal)
+        for j in range(3):
+            scan(["DY%d" % j, "DY", nn], [("wy", h, j)], T.wy[:, 3 * p + 16 * n * j:3 * p + 16 * n * (j + 1)],
+                 T.DY[:, j * C + p:j * C + q], T.nn[:, c], ALU.add, ALU.mult)
         for j in range(2):
-            cps([run], [("Kx", h, j)], T.Kx[:, j * CD + a:j * CD + a + HD], T.run[:, H * h + 15:H * h + H:16])
-        tt([("wy", h, j) for j in range(3)] + [("Yl%d" % j, h) for j in range(3)], [("Yb", h)], T.Yb[:, :, a:a + HD],
-           T.wy[:, 3 * H * h + 15:3 * H * (h + 1):16], T.Yl[:, y:y + 3 * HD], ALU.add)
-        cpv([("Yb", h)], [("o3", h)], T.o3[:, y:y + 3 * HD], T.Yb[:, :, a:a + HD])
-        for j in (1, 2, 0):
-            d = slice(j * C + H * h, j * C + H * h + H)
-            tt(["X", ("o3", h), ai], [("D3", j, h)], T.D3[:, d], XT.indirect(T.o3[:, y + j * HD:y + (j + 1) * HD]),
+            cps([run], [("Kx", h, j)], T.Kx[:, j * CD + a:j * CD + b], T.run[:, p + 15:q:16])
+        tt([("wy", h, j) for j in range(3)] + [("Yl%d" % j, h) for j in range(3)], [("Yb", h)], T.Yb[:, :, a:b],
+           T.wy[:, 3 * p + 15:3 * q:16], T.Yl[:, y:y + 3 * n], ALU.add)
+        cpv([("Yb", h)], [("o3", h)], T.o3[:, y:y + 3 * n], T.Yb[:, :, a:b])
+        for j in (0, 1, 2):
+            d = slice(j * C + p, j * C + q)
+            tt(["X", ("o3", h), ai], [("D3", j, h)], T.D3[:, d], XT.indirect(T.o3[:, y + j * n:y + (j + 1) * n]),
                T[ai][:, c], ALU.subtract, "gather")
             if j:
-                act([("D3", j, h)], [("T3", j, h)], T.T3[:, (j - 1) * C + H * h:(j - 1) * C + H * h + H], T.D3[:, d],
-                    ACT.Abs, 0.0, 1.0)
-        ts([("D3", 0, h)], [("T3", 0, h)], T.T3[:, 2 * C + H * h:2 * C + H * h + H], T.D3[:, c], 0.0, ALU.is_le)
+                act([("D3", j, h)], [("T3", j, h)], T.T3[:, (j - 1) * C + p:(j - 1) * C + q], T.D3[:, d], ACT.Abs, 0.0, 1.0)
+        act([("D3", 0, h)], [("T3", 0, h)], T.T3[:, 2 * C + p:2 * C + q], T.D3[:, c], ACT.Sign, 0.5, -1.0)
 
     for t in range(TS):
         mi, ai, mo, ao = "mi%d" % t, "ai%d" % t, "mo%d" % t, "ao%d" % t
@@ -345,9 +360,12 @@ def rank_program(g, core, T, topo):
             first = "gob" if t > 0 else "zer"
             mm(["diag", first], [("pW", "pB")[h]], T[("pW", "pB")[h]][:, 0:H], T.diag[:, 0:128], T[first][:, H * h:H * h + H],
                True, False)
-        ts(["Rf"], ["pD1"], T.pD[:, C:2 * C], R, -HALF, ALU.add)
-        cpv(["Rf", "onx"], ["Rn"], T.Rn[:], R.indirect(T.onx[:]), "gather")
-        tt(["Rn", "pD1"], ["i3"], T.i3[:], T.Rn[:], T.pD[:, C:2 * C], ALU.subtract)
+        if OPT[0]:
+            act(["Rf"], ["pD1"], T.pR[:, 0:C], R, ACT.Identity, -HALF, 1.0)
+        else:
+            ts(["Rf"], ["pD1"], T.pR[:, 0:C], R, -HALF, ALU.add)
+        (cps if OPT[1] else cpv)(["Rf", "onx"], ["Rn"], T.Rn[:], R.indirect(T.onx[:]), "gather")
+        tt(["Rn", "pD1"], ["i3"], T.i3[:], T.Rn[:], T.pR[:, 0:C], ALU.subtract)
         ts(["i3"], ["i4"], T.i4[:], T.i3[:], W - 1, ALU.bitwise_and)
         ts(["i4"], ["pD0"], T.pD[:, 0:C], T.i4[:], 1.0 / 256, ALU.mult)
         tt(["Rf", "Rn", "DY"], ["DY1"], T.DY[:, C + 1:2 * C:2], T.Rf[:, 0:C:2], T.Rn[:, 1:C:2], ALU.subtract)
@@ -356,14 +374,18 @@ def rank_program(g, core, T, topo):
         for e, a, b in R_CH:
             (cpv if e == "V" else cps)(["X", mi], blocks("G", a, b), T.G[:, 256 * a:256 * b],
                                        XT.indirect(M[:, 16 * a:16 * b]), "gather")
-            behind(*[("G", x) for y, x, z in R_CH if x < a])
+            behind(*([("G", x) for y, x, z in R_CH if x < a] + (["nb"] if a >= HD else [])))
         for h in range(2):
             a, b = HD * h, HD * h + HD
             diagonal("G", "BW", ("pW", "pB")[h], a, b)
-            cps([ai], blocks("Ab", a, b), T.Ab[:, a:b, 0:16], A[:, 16 * a:16 * b])
-            behind(("G", CD - 1), ("G", HD - 1))
+            cp = cpg if h == 0 and t > 0 else cps
+            cp([ai], blocks("Ab", a, b), T.Ab[:, a:b, 0:16], A[:, 16 * a:16 * b])
+            if t > 0:
+                behind(("G", CD - 1), ("G", HD - 1), "Rn", "pD1")
+            else:
+                behind("r2", "diag", "pc4")
             for n in (16, 32, 64, 128):
-                cps(blocks("Ab", a, b), blocks("Ab", a, b), T.Ab[:, a:b, n:2 * n], T.Ab[:, a:b, 0:n])
+                cp(blocks("Ab", a, b), blocks("Ab", a, b), T.Ab[:, a:b, n:2 * n], T.Ab[:, a:b, 0:n])
         for h in range(2):
             probes(t, h)
         for h in range(2):
@@ -371,27 +393,31 @@ def rank_program(g, core, T, topo):
 
         Yb = [("Yb", 0), ("Yb", 1)]
         for r in range(16):
-            mm([("T3", j, h) for j in range(3) for h in range(2)] + ["BE"], ["p3"], T.p3[:, 0:3 * CD],
-               T.BE[:, 15 - r:143 - r], T.T3[:, r:3 * C:16], r == 0, r == 15)
+            mm([("T3", 0, h) for h in range(2)] + ["BE"], ["pN", "order 3"], T.pN[:, 0:CD],
+               T.BE[:, 15 - r:143 - r], T.T3[:, 2 * C + r:3 * C:16], r == 0, r == 15)
+        for r in range(16):
+            mm([("T3", j, h) for j in (1, 2) for h in range(2)] + ["BE"], ["p3", "order 3"], T.p3[:, 0:2 * CD],
+               T.BE[:, 15 - r:143 - r], T.T3[:, r:2 * C:16], r == 0, r == 15)
+        ts(["pN"], ["F0"], T.F[:, 0:CD], T.pN[:, 0:CD], 2048.0, ALU.is_gt, -4 * BIG, ALU.mult)
+        ts(["pN"], ["F1"], T.F[:, CD:2 * CD], T.pN[:, 0:CD], 2048.0, ALU.is_lt, -4 * BIG, ALU.mult)
+        tt(["F0", "F1"] + [("Kx", h, j) for h in range(2) for j in range(2)], ["Ky"], T.Ky[:], T.F[:], T.Kx[:], ALU.add)
         cps(Yb, ["rp"], T.rp[:], T.Yb[:, 1:3, :])
         act(Yb, ["ee"], T.ee[:], T.Yb[:, 1:3, :], ACT.Identity, float(PAD), 1.0)
         tt(["rp", "opa", "Rf"], ["mm"], T.mm[:], T.rp[:].indirect(T.opa[:]), R, ALU.is_equal, "gather")
-        tt(Yb, ["dl0"], T.dl[:, 0:CD], T.Yb[:, 0, :], T.Yb[:, 1, :], ALU.subtract)
-        tt(Yb, ["dl1"], T.dl[:, CD:2 * CD], T.Yb[:, 0, :], T.Yb[:, 2, :], ALU.subtract)
+        cps(Yb, ["q0"], T.te[:, 0:CD], T.Yb[:, 0, :])
+        cps(Yb, ["q1"], T.te[:, CD:2 * CD], T.Yb[:, 0, :])
+        tt(["q0", "q1", "rp"], ["dl0", "dl1", "te"], T.dl[:], T.te[:], T.rp[:], ALU.subtract)
         ts([("D3", 0, 0), ("D3", 0, 1)], ["c3"], T.c3[:], T.D3[:, 0:C], -3.0, ALU.max, 3.0, ALU.min)
-        tt(["p3", "Kx2"] + [("Kx", h, j) for h in range(2) for j in range(2)], ["F"], T.F[:], T.p3[:, 0:3 * CD], T.Kx[:],
-           ALU.is_lt)
-        tt(["F"], ["gg0"], T.gg[:, 0:CD], T.F[:, 0:CD], T.F[:, 2 * CD:3 * CD], ALU.mult)
-        tt(["F"], ["gg1"], T.gg[:, CD:2 * CD], T.F[:, CD:2 * CD], T.F[:, 2 * CD:3 * CD], ALU.is_gt)
+        tt(["p3", "Ky"], ["gg0", "gg1"], T.gg[:], T.p3[:, 0:2 * CD], T.Ky[:], ALU.is_lt)
         KA, KU = T.ka[:, 0:CD], T.ku[:, 0:CD]
         tt(["dl0", "dl1", "opa", "mm"], ["cand"], T.cand[:], T.dl[:].indirect(T.opa[:]), T.mm[:], ALU.mult, "gather")
         tt(["gg0", "gg1", "ee"], ["te"], T.te[:], T.gg[:], T.ee[:], ALU.mult)
         tt(["gg0", "gg1", "opa", "cand"], ["rr"], T.rr[:], T.gg[:].indirect(T.opa[:]), T.cand[:], ALU.mult, "gather")
-        tt(["gg0", "gg1"], ["MF1"], T.MF[:, C:C + CD], T.gg[:, 0:CD], T.gg[:, CD:2 * CD], ALU.add)
         tt(["te"], ["ka"], KA, T.te[:, 0:CD], T.te[:, CD:2 * CD], ALU.add)
+        act(["ka"], ["MF1"], T.MF[:, C:C + CD], KA, ACT.Sign, 0.0, 1.0)
         tt(["te"], ["ke"], T.ka[:, CD:CD + HD], T.te[:, 0:CD:2], T.te[:, CD:2 * CD:2], ALU.add)
         cpv(["ka", "ke"], ["ku"], T.ku[:], T.ka[:])
-        tt(["rr", "pD1"], ["MF0"], T.MF[:, 0:C], T.pD[:, C:2 * C], T.rr[:], ALU.add)
+        tt(["rr", "pD1"], ["MF0"], T.MF[:, 0:C], T.pR[:, 0:C], T.rr[:], ALU.add)
         ts(["MF0", "MF1"], [mo], T[mo][:], T.MF[:], HALF, ALU.add)
         send(mo, "mi%d" % (t + 1), "rm%d" % (t + 1), t)
 
@@ -421,13 +447,15 @@ def rank_program(g, core, T, topo):
     mi, ai = "mi%d" % TS, "ai%d" % TS
     dma("Y", "ox", ["X"], [], T.yx[:], XT)
     dma("S", "oa", [ai], [], T.ya[:], T[ai][:])
-    cpv([mi], ["sa0", "sa1"], T.sa[:], T[mi][:, 0:C])
-    for a, b in (("sa", "sb"), ("sb", "sa")) * 2:
-        for j, o in ((0, ALU.min), (1, ALU.max)):
-            tt([a + "0", a + "1"], [b + str(j)], T[b][:, :, j:16:2], T[a][:, :, 0:8], T[a][:, :, 8:16], o)
-    turn(T.sa[:], ["sa0", "sa1"], T.r1[:], "r1")
-    dma("Y", "orr", ["r1"], [], T.yr[:], T.r1[:])
-    tt(["sb0", "sb1"], ["sf"], T.sf[:, 0:CD], T.sb[:, :, 0], T.sb[:, :, 8], ALU.is_lt)
+    for h in range(2):
+        s = slice(HD * h, HD * h + HD)
+        cpv([mi], [("sa", 0, h), ("sa", 1, h)], T.sa[:, s, :], T[mi][:, H * h:H * h + H])
+        for a, b in (("sa", "sb"), ("sb", "sa")) * 2:
+            for j, o in ((0, ALU.min), (1, ALU.max)):
+                tt([(a, 0, h), (a, 1, h)], [(b, j, h)], T[b][:, s, j:16:2], T[a][:, s, 0:8], T[a][:, s, 8:16], o)
+        turn(T.sa[:, s, :], [("sa", 0, h), ("sa", 1, h)], T.r1[:, H * h:H * h + H], ("r1", h), h)
+    dma("Y", "orr", blocks("r1", 0, 2), [], T.yr[:], T.r1[:])
+    tt([("sb", j, h) for j in range(2) for h in range(2)], ["sf"], T.sf[:, 0:CD], T.sb[:, :, 0], T.sb[:, :, 8], ALU.is_lt)
     tt(["sf", "ob", "diag"], ["sx"], T.sx[:], T.sf[:].indirect(T.ob[:]), T.diag[:], ALU.mult, "gather")
     mm(["E8", "sx"], ["pA"], T.pA[0:8, 0:C], T.E8[:], T.sx[:], True, True)
     act(["pA"], ["so"], T.so[0:8, :], T.pA[0:8, 0:C], ACT.Identity, -1.0, 2.0)

from concourse.mybir import AluOpType, ActivationFunctionType

ALU = AluOpType
ACT = ActivationFunctionType
W, C, TS, HOP = 4096, 192, 5, 3
CD = C // 16
H, HD = C // 2, CD // 2
PAD = 48
BIG = 16777216.0
HALF = 255.0 / 512
F32, BF, I32, U16 = "float32", "bfloat16", "int32", "uint16"

SCRATCH = {"Ab": ("sbuf", [128, CD, 256], BF), "u": ("sbuf", [128, CD, 17], I32), "Yb": ("sbuf", [128, 3, CD], F32),
           "Z": ("sbuf", [128, CD, 32], F32), "Zt": ("sbuf", [128, CD, 32], F32),
           "sa": ("sbuf", [128, CD, 16], F32), "sb": ("sbuf", [128, CD, 16], F32)}
for _names, _n, _d in (
        ("X", W + PAD, BF), ("IOT", W + PAD, F32), ("G D DA", 16 * C, BF),
        ("ti", 8, I32), ("pf pc", 8, F32), ("ps", 5, F32), ("oc", HD, U16), ("Ne n2 n3", H, F32), ("cand", C, F32),
        ("ka", CD + HD, F32), ("ku", CD + HD, U16), ("kb", CD, F32), ("wi", 1, I32),
        ("cp chi negI SH pm1", 128, F32), ("vI E8T", 128, BF), ("colf", 144, F32), ("k1", 152, F32), ("BW BE", 144, BF),
        ("E8", 8, BF), ("w01", 16, BF), ("sf", 16, F32), ("ob opa onx lo", CD, U16),
        ("colm m8 rsn rs1 r1 r2 r3 so Rn nb dh run nn mm rr Nm ne nd", C, F32),
        ("diag zer sgb sx gob vo c3 ta xl dx c4 c5", C, BF), ("rli sgi i1 i2 i3 i4 qi", C, I32), ("qu", C, U16),
        ("Rf MF", C + CD, F32), ("DY wy", 3 * C, F32), ("D3 T3", 3 * C, BF),
        ("Yl", 3 * CD, F32), ("o3", 3 * CD, U16), ("gg dl ee te rp Kx Ky F", 2 * CD, F32), ("kn", CD, F32),
        ("mi0 mi1 mi2 mi3 mi4 mi5", C + CD, U16),
        ("mo0 mo1 mo2 mo3 mo4", C + CD, U16),
        ("ai0 ai1 ai2 ai3 ai4 ai5 ao0 ao1 ao2 ao3 ao4", C, BF)):
    for _x in _names.split():
        SCRATCH[_x] = ("sbuf", [128, _n], _d)
PSUM = ("pW", "pK", "p3", "pN", "pA", "pB")
for _x in PSUM + ("pD", "pR"):
    SCRATCH[_x] = ("psum", [128, 512], F32)

SEMAPHORES = (["cV", "cS", "cP", "cG", "sent", "lx", "lr", "la", "ls", "lw", "ox", "oa", "orr", "osg"]
              + ["rm%d" % t for t in range(1, TS + 1)] + ["ra%d" % t for t in range(1, TS + 1)])

R_CH = [("V", 0, 3), ("S", 3, 6), ("V", 6, 8), ("S", 8, 12)]
OPT = [1, 0, 0]
PARTS = [(0, 8), (8, 12)]
ABS_CH = [(0, 2), (2, 4), (4, 6), (6, 8), (8, 10), (10, 11), (11, 12)]
CYCLE, PE_CYCLE, WAKE, SLACK, FLIGHT = 0.9, 0.6, 160.0, 20.0, 3500.0
SPREAD, SALT = 0.0, 1


def rank_program(g, core, T, topo):
    rank = T.rank_of(core)
    if rank is None:
        return
    N = len(T.cores)
    Q = {"V": g.vector, "S": g.scalar, "P": g.tensor, "G": g, "Y": g.sync}
    ops = []
    writer = {}
    readers = {}

    def add(e, reads, writes, call, cost, lat=0.0, sem=None, inc=1):
        deps = set()
        for k in list(reads) + list(writes):
            if k in writer:
                deps.add(writer[k])
        for k in writes:
            deps.update(readers.get(k, []))
        for k in reads:
            if k in PSUM:
                deps.update(i for i in readers.get(k, []) if ops[i]["e"] != e)
        ops.append({"e": e, "deps": deps, "call": call, "cost": cost, "lat": lat, "sem": sem, "inc": inc, "soft": set()})
        for k in writes:
            writer[k] = len(ops) - 1
            readers[k] = []
        for k in reads:
            if k not in writes:
                readers.setdefault(k, []).append(len(ops) - 1)

    def behind(*keys):
        o = ops[-1]
        o["soft"] = {writer[k] for k in keys if k in writer and ops[writer[k]]["e"] == o["e"]} - o["deps"] - {len(ops) - 1}
        o["deps"] = o["deps"] | o["soft"]

    def emit():
        n = len(ops)
        after = [[] for _ in range(n)]
        for i, o in enumerate(ops):
            for d in o["deps"]:
                after[d].append(i)

        def gap(d, i):
            if d in ops[i]["soft"] or (ops[d]["e"] == "P" and ops[i]["e"] == "P"):
                return 0.0
            return ops[d]["lat"] + WAKE
        tail = [0.0] * n
        for i in range(n - 1, -1, -1):
            tail[i] = ops[i]["cost"] + max([gap(i, j) + tail[j] for j in after[i]] + [ops[i]["lat"]])
        for i in range(n):
            tail[i] += SPREAD * ((i * SALT) % 1009) / 1009.0
        left = [len(o["deps"]) for o in ops]
        ready_at = [0.0] * n
        ready = [i for i in range(n) if left[i] == 0]
        free, known, final, mark = {}, {}, {}, {}
        while ready:
            start = {i: max(ready_at[i], free.get(ops[i]["e"], 0.0)) for i in ready}
            first = min(ready, key=lambda i: (start[i], -tail[i], i))
            e = ops[first]["e"]
            i = max((j for j in ready if ops[j]["e"] == e and start[j] <= start[first] + SLACK), key=lambda j: (tail[j], -j))
            o = ops[i]
            ready.remove(i)
            end = start[i] + o["cost"]
            s = o["sem"] or "c" + e
            final[s] = final.get(s, 0) + o["inc"]
            mark[i] = (s, final[s])
            if e != "F":
                free[e] = end
                need = {}
                for d in o["deps"] - o["soft"]:
                    if not (e == "P" and ops[d]["e"] == "P"):
                        need[mark[d][0]] = max(need.get(mark[d][0], 0), mark[d][1])
                for w, v in need.items():
                    if known.get((e, w), 0) < v:
                        known[(e, w)] = v
                        Q[e].wait_ge(T.sem[w], v)
                done = o["call"]()
                if s != "sent":
                    done.then_inc(T.sem[s], o["inc"])
            for j in after[i]:
                ready_at[j] = max(ready_at[j], end + gap(i, j))
                left[j] -= 1
                if left[j] == 0:
                    ready.append(j)
        for s, v in final.items():
            g.wait_ge(T.sem[s], v)

    def size(ap):
        n = 1
        for x in ap.shape[1:]:
            n *= x
        return n

    def price(out, per, kind=None):
        if kind == "scatter":
            return 50.0 + 32 * 3.8 * CYCLE
        if kind == "gather":
            return 50.0 + size(out) * 1.56 * CYCLE
        return 60.0 + max(64, size(out) * per) * CYCLE

    def dma(e, sem, reads, writes, out, in_, slow=False):
        def call():
            if slow:
                return Q[e].dma_start(out, in_, allow_slow_non_contiguous=True)
            return Q[e].dma_start(out, in_)
        add(e, reads, writes, call, 100.0, 2000.0 + 0.6 * size(out), sem, 16)

    def lanes(src, dst):
        m = 0
        es = topo.engines(src, dst)[:8]
        for x in es:
            m |= 1 << x
        return m, len(es)

    def send(name, there, sem, t):
        hop = HOP if t < TS - 1 else -HOP * t
        dst, src = T.cores[(rank + hop) % N], T.cores[(rank - hop) % N]
        rid, pid, _ = topo.addr(dst)
        m, n = lanes(core, dst)
        add("G", [name], ["sent " + name],
            lambda: g.remote_dma(T[there][:], T[name][:, 0:T[there].shape[1]], T.sem[sem], T.sem.sent, pid, rid, m),
            500.0, 0.0, "sent", n)
        add("F", ["sent " + name], [there], None, FLIGHT, 0.0, sem, lanes(src, core)[1])

    def tt(r, w, out, a, b, o, kind=None):
        both = 1 if any(k in PSUM or k in ("pD0", "pD1") for k in r) else 2
        add("V", r, w, lambda: g.vector.tensor_tensor(out, a, b, o), price(out, both, kind))

    def ts(r, w, out, a, s1, o1, s2=None, o2=None):
        if o2 is None:
            add("V", r, w, lambda: g.vector.tensor_scalar(out, a, s1, None, o1), price(out, 1))
        else:
            add("V", r, w, lambda: g.vector.tensor_scalar(out, a, s1, s2, o1, o2), price(out, 1))

    def cpv(r, w, out, a, kind=None):
        add("V", r, w, lambda: g.vector.tensor_copy(out, a), price(out, 1, kind))

    def cps(r, w, out, a, kind=None):
        add("S", r, w, lambda: g.scalar.activation(out, a, ACT.Copy), price(out, 1, kind))

    def cpg(r, w, out, a):
        add("G", r, w, lambda: g.affine_select(out, a, [[0, size(out)]], ALU.is_gt, 0.0, 1, 0), 170.0 + 2 * size(out) * CYCLE)

    def act(r, w, out, a, func, bias, scale, kind=None):
        add("S", r, w, lambda: g.scalar.activation(out, a, func, bias=bias, scale=scale), price(out, 1, kind))

    def mset(w, out, val):
        add("V", [], w, lambda: g.vector.memset(out, val), price(out, 0.5))

    def scan(r, w, out, d0, d1, o0, o1):
        add("V", r, w, lambda: g.vector.tensor_tensor_scan(out, d0, d1, 0.0, o0, o1), price(out, 1))

    def mm(r, w, out, lhsT, rhs, start, stop, wide=1):
        add("P", r, w, lambda: g.tensor.matmul(out, lhsT, rhs, start, stop), max(64, size(out)) * wide * PE_CYCLE)

    def iota(w, out, pattern, base, mult):
        add("G", [], w, lambda: g.iota(out, pattern, base, mult, allow_small_or_imprecise_dtypes=True),
            130.0 + 2 * size(out) * CYCLE)

    def blocks(name, a, b):
        return [(name, i) for i in range(a, b)]

    def turn(src, src_keys, dst, dst_key, h):
        s = slice(HD * h, HD * h + HD)
        ts(src_keys + ["pc4"], [("Z0", h)], T.Z[:, s, 0:16], src, T.pc[:, 4:5], ALU.mult)
        act(src_keys + ["pf"], [("Z1", h)], T.Z[:, s, 16:32], src, ACT.Identity, 0.0, T.pf[:, 3:4])
        add("V", [("Z0", h), ("Z1", h)], [("Zt", h)], lambda: g.vector.transpose(T.Zt[:, s, :], T.Z[:, s, :]),
            price(T.Zt[:, s, :], 1))
        tt([("Zt", h)], [dst_key], dst, T.Zt[:, s, 0:16], T.Zt[:, s, 16:32], ALU.add)

    def diagonal(name, B, out, a, b):
        for r in range(16):
            mm(blocks(name, a, b) + [B], [out, "order " + B], T[out][:, 0:16 * (b - a)], T[B][:, 15 - r:143 - r],
               T[name][:, 256 * a + r:256 * b:16], False, r == 15)

    XT = T.X[:, PAD:PAD + W]
    R = T.Rf[:, 0:C]

    dma("S", "lr", [], ["rli"], T.rli[:], T.rl[:])
    dma("Y", "ls", [], ["sgi"], T.sgi[0:8, :], T.sg[:])
    dma("Y", "lx", [], ["X"], XT, T.xt[:])
    dma("S", "la", [], ["ai0"], T.ai0[:], T.av[:])
    dma("G", "lw", [], ["wi"], T.wi[:], T.wt[:], slow=True)
    add("G", [], ["ti0"], lambda: g.iota(T.ti[:, 0:1], [[0, 1]], 0, 1), 130.0)
    iota(["colf"], T.colf[:], [[1, 144]], 0, 0)
    iota(["cp"], T.cp[:], [[1, 128]], 0, -1)
    iota(["chi"], T.chi[0:8, :], [[1, 8], [0, 16]], 0, -1)
    iota(["colm"], T.colm[:], [[0, CD], [1, 16]], 0, 0)
    iota(["DY"], T.DY[:], [[0, 3 * C]], 0, 0)
    iota(["w01"], T.w01[:], [[1, 16]], 0, 0)
    iota(["sf"], T.sf[:], [[0, 16]], 0, 0)
    iota(["IOT"], T.IOT[:], [[1, W + PAD]], 0, 0)
    behind("ti0", "colf", "cp", "chi", "colm", "DY", "Kx2", "w01", "sf")
    mset(["Xpad"], T.X[:, 0:PAD], 0.0)
    mset(["zer"], T.zer[:], 0.0)
    ts(["ti0"], ["ti1"], T.ti[:, 1:2], T.ti[:, 0:1], 15, ALU.bitwise_and)
    ts(["ti0"], ["ti2"], T.ti[:, 2:3], T.ti[:, 0:1], 4, ALU.logical_shift_right)
    ts(["ti0"], ["ti3"], T.ti[:, 3:4], T.ti[:, 0:1], 4, ALU.logical_shift_right, 1, ALU.bitwise_and)
    ts(["ti0"], ["ti4"], T.ti[:, 4:5], T.ti[:, 0:1], 1, ALU.bitwise_and)
    cpv(["ti0", "ti1", "ti2", "ti3", "ti4"], ["pf"], T.pf[:, 0:5], T.ti[:, 0:5])
    ts(["pf"], ["pc1"], T.pc[:, 1:2], T.pf[:, 1:2], 0.0, ALU.is_equal, 16.0, ALU.mult)
    ts(["cp"], ["negI"], T.negI[:], T.cp[:], 0.0, ALU.is_equal, -1.0, ALU.mult)
    ts(["pf", "pc1"], ["pc5"], T.pc[:, 5:6], T.pf[:, 0:1], T.pc[:, 1:2], ALU.add, -1.0, ALU.add)
    ts(["chi"], ["E8T"], T.E8T[0:8, :], T.chi[0:8, :], 0.0, ALU.is_equal)
    ts(["colf", "pc5"], ["pm1"], T.pm1[:], T.colf[:, 0:128], T.pc[:, 5:6], ALU.is_equal)
    act(["pf"], ["pc0"], T.pc[:, 0:1], T.pf[:, 2:3], ACT.Identity, 15.0, 16.0)
    act(["pf"], ["pc2"], T.pc[:, 2:3], T.pf[:, 1:2], ACT.Identity, 1.0, 1.0)
    act(["pf"], ["pc3"], T.pc[:, 3:4], T.pf[:, 4:5], ACT.Identity, 0.0, float(CD))
    act(["pf"], ["pc4"], T.pc[:, 4:5], T.pf[:, 3:4], ACT.Identity, 1.0, -1.0)
    act(["pf"], ["ps0"], T.ps[:, 0:1], T.pf[:, 1:2], ACT.Identity, 0.0, -1.0)
    act(["pf"], ["ps1"], T.ps[:, 1:2], T.pf[:, 1:2], ACT.Identity, 8192.0, -8192.0)
    act(["pf"], ["ps2"], T.ps[:, 2:3], T.pf[:, 2:3], ACT.Identity, -15.0, -16.0)
    act(["pf"], ["ps3"], T.ps[:, 3:4], T.pf[:, 2:3], ACT.Identity, 0.0, -1.0)
    tt(["pm1", "negI"], ["SH"], T.SH[:], T.pm1[:], T.negI[:], ALU.add)
    ts(["pf"], ["pc7"], T.pc[:, 7:8], T.pf[:, 1:2], 15.0, ALU.is_lt)
    cpv(["wi"], ["wf"], T.pf[:, 5:6], T.wi[:])
    ts(["pc2", "pc7"], ["pc6"], T.pc[:, 6:7], T.pc[:, 2:3], T.pc[:, 7:8], ALU.mult)
    ts(["colf", "pc0", "wf"], ["BW"], T.BW[:], T.colf[:], T.pc[:, 0:1], ALU.is_equal, T.pf[:, 5:6], ALU.mult)
    ts(["colf"], ["ob"], T.ob[:], T.colf[:, 0:CD], 0.0, ALU.add)
    ts(["colf"], ["oc"], T.oc[:], T.colf[:, 0:HD], 2.0, ALU.mult, 1.0, ALU.add)
    act(["pf"], ["ps4"], T.ps[:, 4:5], T.pf[:, 1:2], ACT.Identity, 17.0, 1.0)
    ts(["colf", "pc3"], ["opa"], T.opa[:], T.colf[:, 0:CD], T.pc[:, 3:4], ALU.add)
    ts(["colf", "pc6"], ["onx"], T.onx[:], T.colf[:, 0:CD], 16.0, ALU.mult, T.pc[:, 6:7], ALU.add)
    act(["colf", "ps2"], ["k1"], T.k1[:, 0:144], T.colf[:], ACT.Abs, T.ps[:, 2:3], 1.0)
    act(["colm", "ps0"], ["Nm"], T.Nm[:], T.colm[:], ACT.Abs, T.ps[:, 0:1], 1.0)
    act(["colf", "ps3"], ["k3"], T.k1[:, 144:152], T.colf[:, 0:8], ACT.Abs, T.ps[:, 3:4], 1.0)
    act(["colm"], ["rs1"], T.rs1[:], T.colm[:], ACT.Relu, 1.0, -1.0)
    act(["k1"], ["BE"], T.BE[:], T.k1[:, 0:144], ACT.Relu, 4096.0, -4096.0)
    act(["Nm"], ["diag"], T.diag[:], T.Nm[:], ACT.Relu, 1.0, -1.0)
    act(["k3"], ["E8"], T.E8[:], T.k1[:, 144:152], ACT.Relu, 1.0, -1.0)
    act(["rs1"], ["rsn"], T.rsn[:], T.rs1[:], ACT.Identity, 0.0, -1e20)
    act(["negI"], ["vI"], T.vI[:], T.negI[:], ACT.Identity, 0.0, BIG)
    act(["colm", "ps1"], ["m8"], T.m8[:], T.colm[:], ACT.Relu, T.ps[:, 1:2], 8192.0)
    ts(["sgi"], ["sgb"], T.sgb[0:8, :], T.sgi[0:8, :], 0.0, ALU.is_lt)
    cpv(["rli"], ["r1"], T.r1[:], T.rli[:])
    mm(["E8T", "sgb"], ["pB"], T.pB[:, 0:C], T.E8T[0:8, :], T.sgb[0:8, :], True, True)
    mm(["SH", "r1"], ["pA"], T.pA[:, 0:C], T.SH[:], T.r1[:], True, True, 4)
    cps(["pB"], ["r2"], T.r2[:], T.pB[:, 0:C])
    for h in range(2):
        c = slice(H * h, H * h + H)
        tt(["pA", "r2"], [("r3", h)], T.r3[:, c], T.pA[:, c], T.r2[:, c], ALU.mult)
        tt([("r3", h), "r1"], [("so", h)], T.so[:, c], T.r3[:, c], T.r1[:, c], ALU.add)
        turn(T.so[:, c], [("so", h)], T.r3[:, c], ("r3", h), h)
    cpv(blocks("r3", 0, 2), ["mi0"], T.mi0[:, 0:C], T.r3[:])
    cps(blocks("r3", 0, 2), ["Rf"], R, T.r3[:])

    def probes(t, h):
        c, b, pw, pk = slice(H * h, H * h + H), slice(HD * h, HD * h + HD), ("pW", "pB")[h], ("pK", "pA")[h]
        i1, i2, u0, u1, dh, qi, qu, vo = [(x, h) for x in ("i1", "i2", "u0", "u1", "dh", "qi", "qu", "vo")]
        Wh = T[pw][:, 0:H]
        if t > 0:
            tt([pw, "nb"], [i1], T.i1[:, c], Wh, T.nb[:, c], ALU.subtract)
        else:
            cpv([pw], [i1], T.i1[:, c], Wh)
        ts([i1], [u0], T.u[:, b, 0:16], T.i1[:, c], W - 1, ALU.bitwise_and)
        ts([i1], [u1], T.u[:, b, 16], T.i1[:, H * h:H * h + H:16], W - 1, ALU.bitwise_and)
        tt([u0, u1], [i2], T.i2[:, c], T.u[:, b, 0:16], T.u[:, b, 1:17], ALU.mult)
        ts([i2], [i1], T.i1[:, c], T.i2[:, c], 5, ALU.logical_shift_right)
        tt([i1, pw], [i2], T.i2[:, c], Wh, T.i1[:, c], ALU.add)
        ts([i2], [i1], T.i1[:, c], T.i2[:, c], 255, ALU.bitwise_and)
        tt([i1, "pD0"], [dh], T.dh[:, c], T.pD[:, c], T.i1[:, c], ALU.mult)
        tt([dh, "pD1"], [i2], T.i2[:, c], T.pR[:, c], T.dh[:, c], ALU.add)
        ts([i2], [qi], T.qi[:, c], T.i2[:, c], W - 1, ALU.bitwise_and)
        cpv([qi], [qu], T.qu[:, c], T.qi[:, c])
        act([dh], [vo], T.vo[:, c], T.dh[:, c], ACT.Relu, 256.0, -256.0)

    def choose(t, h):
        ai = "ai%d" % t
        a, b = PARTS[h]
        n, p, q, pk = b - a, 16 * a, 16 * b, ("pK", "pA")[h]
        c, key = slice(p, q), T[pk][:, 0:16 * n]
        y, qi, run, nn = 3 * a, blocks("qi", 0, 2), ("run", h), ("nn", h)
        mm(["negI", "Rf"], [pk], key, T.negI[:], T.Rf[:, c], True, False, 4)
        mm(["vI"] + blocks("vo", 0, 2), [pk], key, T.vI[:], T.vo[:, c], False, False)
        for cd in range(a, b):
            tt(["X", ("qu", cd // HD), ("Ab", cd)], [("D", cd)], T.D[:, 256 * cd:256 * cd + 256],
               XT.indirect(T.qu[:, 16 * cd:16 * cd + 16]), T.Ab[:, cd, :], ALU.subtract, "gather")
            if OPT[2]:
                behind(("D", cd - 1))
        for r, s in ABS_CH:
            if a <= r < b:
                act(blocks("D", r, s), blocks("DA", r, s), T.DA[:, 256 * r:256 * s], T.D[:, 256 * r:256 * s], ACT.Abs, 0.0, 1.0)
        diagonal("DA", "BE", pk, a, b)
        if h == 0:
            tt(qi + ["DY"], ["DY0"], T.DY[:, 1:C], T.qi[:, 0:C - 1], T.qi[:, 1:C], ALU.subtract)
        cpv(qi, [("Yl0", h)], T.Yl[:, y:y + n], T.qi[:, p + 15:q:16])
        cps(["Rf"], [("Yl1", h)], T.Yl[:, y + n:y + 2 * n], T.Rf[:, p:q:16])
        cps(["Rf"], [("Yl2", h)], T.Yl[:, y + 2 * n:y + 3 * n], T.Rf[:, p + 15:q:16])
        scan(["rsn", pk], [run], T.run[:, c], T.rsn[:, c], key, ALU.add, ALU.max)
        tt([pk, run], [nn], T.nn[:, c], key, T.run[:, c], ALU.not_equal)
        for j in range(3):
            scan(["DY%d" % j, "DY", nn], [("wy", h, j)], T.wy[:, 3 * p + 16 * n * j:3 * p + 16 * n * (j + 1)],
                 T.DY[:, j * C + p:j * C + q], T.nn[:, c], ALU.add, ALU.mult)
        for j in range(2):
            cps([run], [("Kx", h, j)], T.Kx[:, j * CD + a:j * CD + b], T.run[:, p + 15:q:16])
        tt([("wy", h, j) for j in range(3)] + [("Yl%d" % j, h) for j in range(3)], [("Yb", h)], T.Yb[:, :, a:b],
           T.wy[:, 3 * p + 15:3 * q:16], T.Yl[:, y:y + 3 * n], ALU.add)
        cpv([("Yb", h)], [("o3", h)], T.o3[:, y:y + 3 * n], T.Yb[:, :, a:b])
        for j in (0, 1, 2):
            d = slice(j * C + p, j * C + q)
            tt(["X", ("o3", h), ai], [("D3", j, h)], T.D3[:, d], XT.indirect(T.o3[:, y + j * n:y + (j + 1) * n]),
               T[ai][:, c], ALU.subtract, "gather")
            if j:
                act([("D3", j, h)], [("T3", j, h)], T.T3[:, (j - 1) * C + p:(j - 1) * C + q], T.D3[:, d], ACT.Abs, 0.0, 1.0)
        act([("D3", 0, h)], [("T3", 0, h)], T.T3[:, 2 * C + p:2 * C + q], T.D3[:, c], ACT.Sign, 0.5, -1.0)

    for t in range(TS):
        mi, ai, mo, ao = "mi%d" % t, "ai%d" % t, "mo%d" % t, "ao%d" % t
        M, A = T[mi], T[ai]

        if t > 0:
            cpv([mi], ["Rf"], T.Rf[:], M[:])
            cps(["Rf", "ob"], ["gob"], T.gob[:], T.Rf[:, C:C + CD].indirect(T.ob[:]), "gather")
            mm(["diag", "gob"], ["pN"], T.pN[:, 0:C], T.diag[:, 0:128], T.gob[:], True, True)
            cps(["pN"], ["nb"], T.nb[:], T.pN[:, 0:C])
        for h in range(2):
            first = "gob" if t > 0 else "zer"
            mm(["diag", first], [("pW", "pB")[h]], T[("pW", "pB")[h]][:, 0:H], T.diag[:, 0:128], T[first][:, H * h:H * h + H],
               True, False)
        if OPT[0]:
            act(["Rf"], ["pD1"], T.pR[:, 0:C], R, ACT.Identity, -HALF, 1.0)
        else:
            ts(["Rf"], ["pD1"], T.pR[:, 0:C], R, -HALF, ALU.add)
        (cps if OPT[1] else cpv)(["Rf", "onx"], ["Rn"], T.Rn[:], R.indirect(T.onx[:]), "gather")
        tt(["Rn", "pD1"], ["i3"], T.i3[:], T.Rn[:], T.pR[:, 0:C], ALU.subtract)
        ts(["i3"], ["i4"], T.i4[:], T.i3[:], W - 1, ALU.bitwise_and)
        ts(["i4"], ["pD0"], T.pD[:, 0:C], T.i4[:], 1.0 / 256, ALU.mult)
        tt(["Rf", "Rn", "DY"], ["DY1"], T.DY[:, C + 1:2 * C:2], T.Rf[:, 0:C:2], T.Rn[:, 1:C:2], ALU.subtract)
        tt(["Rf", "Rn", "DY"], ["DY2"], T.DY[:, 2 * C + 2:3 * C:2], T.Rf[:, 1:C - 1:2], T.Rn[:, 2:C:2], ALU.subtract)

        for e, a, b in R_CH:
            (cpv if e == "V" else cps)(["X", mi], blocks("G", a, b), T.G[:, 256 * a:256 * b],
                                       XT.indirect(M[:, 16 * a:16 * b]), "gather")
            behind(*([("G", x) for y, x, z in R_CH if x < a] + (["nb"] if a >= HD else [])))
        for h in range(2):
            a, b = HD * h, HD * h + HD
            diagonal("G", "BW", ("pW", "pB")[h], a, b)
            cp = cpg if h == 0 and t > 0 else cps
            cp([ai], blocks("Ab", a, b), T.Ab[:, a:b, 0:16], A[:, 16 * a:16 * b])
            if t > 0:
                behind(("G", CD - 1), ("G", HD - 1), "Rn", "pD1")
            else:
                behind("r2", "diag", "pc4")
            for n in (16, 32, 64, 128):
                cp(blocks("Ab", a, b), blocks("Ab", a, b), T.Ab[:, a:b, n:2 * n], T.Ab[:, a:b, 0:n])
        for h in range(2):
            probes(t, h)
        for h in range(2):
            choose(t, h)

        Yb = [("Yb", 0), ("Yb", 1)]
        for r in range(16):
            mm([("T3", 0, h) for h in range(2)] + ["BE"], ["pN", "order 3"], T.pN[:, 0:CD],
               T.BE[:, 15 - r:143 - r], T.T3[:, 2 * C + r:3 * C:16], r == 0, r == 15)
        for r in range(16):
            mm([("T3", j, h) for j in (1, 2) for h in range(2)] + ["BE"], ["p3", "order 3"], T.p3[:, 0:2 * CD],
               T.BE[:, 15 - r:143 - r], T.T3[:, r:2 * C:16], r == 0, r == 15)
        ts(["pN"], ["F0"], T.F[:, 0:CD], T.pN[:, 0:CD], 2048.0, ALU.is_gt, -4 * BIG, ALU.mult)
        ts(["pN"], ["F1"], T.F[:, CD:2 * CD], T.pN[:, 0:CD], 2048.0, ALU.is_lt, -4 * BIG, ALU.mult)
        tt(["F0", "F1"] + [("Kx", h, j) for h in range(2) for j in range(2)], ["Ky"], T.Ky[:], T.F[:], T.Kx[:], ALU.add)
        cps(Yb, ["rp"], T.rp[:], T.Yb[:, 1:3, :])
        act(Yb, ["ee"], T.ee[:], T.Yb[:, 1:3, :], ACT.Identity, float(PAD), 1.0)
        tt(["rp", "opa", "Rf"], ["mm"], T.mm[:], T.rp[:].indirect(T.opa[:]), R, ALU.is_equal, "gather")
        cps(Yb, ["q0"], T.te[:, 0:CD], T.Yb[:, 0, :])
        cps(Yb, ["q1"], T.te[:, CD:2 * CD], T.Yb[:, 0, :])
        tt(["q0", "q1", "rp"], ["dl0", "dl1", "te"], T.dl[:], T.te[:], T.rp[:], ALU.subtract)
        ts([("D3", 0, 0), ("D3", 0, 1)], ["c3"], T.c3[:], T.D3[:, 0:C], -3.0, ALU.max, 3.0, ALU.min)
        tt(["p3", "Ky"], ["gg0", "gg1"], T.gg[:], T.p3[:, 0:2 * CD], T.Ky[:], ALU.is_lt)
        KA, KU = T.ka[:, 0:CD], T.ku[:, 0:CD]
        tt(["dl0", "dl1", "opa", "mm"], ["cand"], T.cand[:], T.dl[:].indirect(T.opa[:]), T.mm[:], ALU.mult, "gather")
        tt(["gg0", "gg1", "ee"], ["te"], T.te[:], T.gg[:], T.ee[:], ALU.mult)
        tt(["gg0", "gg1", "opa", "cand"], ["rr"], T.rr[:], T.gg[:].indirect(T.opa[:]), T.cand[:], ALU.mult, "gather")
        tt(["te"], ["ka"], KA, T.te[:, 0:CD], T.te[:, CD:2 * CD], ALU.add)
        act(["ka"], ["MF1"], T.MF[:, C:C + CD], KA, ACT.Sign, 0.0, 1.0)
        tt(["te"], ["ke"], T.ka[:, CD:CD + HD], T.te[:, 0:CD:2], T.te[:, CD:2 * CD:2], ALU.add)
        cpv(["ka", "ke"], ["ku"], T.ku[:], T.ka[:])
        tt(["rr", "pD1"], ["MF0"], T.MF[:, 0:C], T.pR[:, 0:C], T.rr[:], ALU.add)
        ts(["MF0", "MF1"], [mo], T[mo][:], T.MF[:], HALF, ALU.add)
        send(mo, "mi%d" % (t + 1), "rm%d" % (t + 1), t)

        tt(["w01", mo, "c3"], ["ta"], T.ta[:], T.w01[:].indirect(T[mo][:, C:C + CD]), T.c3[:], ALU.mult, "gather")
        tt(["ta", ai], [ao], T[ao][:], T.ta[:], A[:], ALU.add)
        send(ao, "ai%d" % (t + 1), "ra%d" % (t + 1), t)

        tt(["IOT", "ku", "m8"], ["Nm"], T.Nm[:], T.IOT[:].indirect(KU), T.m8[:], ALU.add, "gather")
        cps(["IOT", "ku"], ["Ne"], T.Ne[:], T.IOT[:].indirect(T.ku[:, CD:CD + HD]), "gather")
        act(["X", "Xpad", "ku"], ["xl"], T.xl[:], T.X[:].indirect(KU), ACT.Identity, -5.0, 1.0, "gather")
        tt(["X", "Xpad", "ku", ai], ["dx"], T.dx[:], T.X[:].indirect(KU), A[:], ALU.subtract, "gather")
        act(["dx"], ["c4"], T.c4[:], T.dx[:], ACT.Relu, 5.0, 1.0)
        act(["c4"], ["c5"], T.c5[:], T.c4[:], ACT.Relu, 10.0, -1.0)
        tt(["ka", "ke", "ob", "Nm"], ["ne"], T.ne[:], T.ka[:].indirect(T.ob[:]), T.Nm[:], ALU.not_equal, "gather")
        tt(["ka", "ke", "oc", "Ne"], ["n2"], T.n2[:], T.ka[:].indirect(T.oc[:]), T.Ne[:], ALU.not_equal, "gather")
        scan(["rs1", "ne"], ["nd"], T.nd[:], T.rs1[:], T.ne[:], ALU.max, ALU.min)
        scan(["rs1", "n2"], ["n3"], T.n3[:], T.rs1[:, 0:H], T.n2[:], ALU.max, ALU.min)
        cps(["ka"], ["kb0"], T.kb[:, 0:CD:2], T.ka[:, 0:CD:2])
        tt(["ka", "n3"], ["kb1"], T.kb[:, 1:CD:2], T.ka[:, 1:CD:2], T.n3[:, 15:H:16], ALU.mult)
        tt(["kb0", "kb1", "nd"], ["kn"], T.kn[:], T.kb[:], T.nd[:, 15:C:16], ALU.mult)
        ts(["kn", "pc2"], ["lo0"], T.lo[:, 0:CD:2], T.kn[:, 0:CD:2], T.pc[:, 2:3], ALU.max)
        ts(["kn", "ps4"], ["lo1"], T.lo[:, 1:CD:2], T.kn[:, 1:CD:2], T.ps[:, 4:5], ALU.max)
        for cd in range(CD - 2, -1, -2):
            tt(["lo0", "lo1", "xl", "c5"], ["X", "Xpad"], T.X[:].indirect(T.lo[:, cd:cd + 2]),
               T.xl[:, 16 * cd:16 * cd + 32], T.c5[:, 16 * cd:16 * cd + 32], ALU.add, "scatter")

    mi, ai = "mi%d" % TS, "ai%d" % TS
    dma("Y", "ox", ["X"], [], T.yx[:], XT)
    dma("S", "oa", [ai], [], T.ya[:], T[ai][:])
    for h in range(2):
        s = slice(HD * h, HD * h + HD)
        cpv([mi], [("sa", 0, h), ("sa", 1, h)], T.sa[:, s, :], T[mi][:, H * h:H * h + H])
        for a, b in (("sa", "sb"), ("sb", "sa")) * 2:
            for j, o in ((0, ALU.min), (1, ALU.max)):
                tt([(a, 0, h), (a, 1, h)], [(b, j, h)], T[b][:, s, j:16:2], T[a][:, s, 0:8], T[a][:, s, 8:16], o)
        turn(T.sa[:, s, :], [("sa", 0, h), ("sa", 1, h)], T.r1[:, H * h:H * h + H], ("r1", h), h)
    dma("Y", "orr", blocks("r1", 0, 2), [], T.yr[:], T.r1[:])
    tt([("sb", j, h) for j in range(2) for h in range(2)], ["sf"], T.sf[:, 0:CD], T.sb[:, :, 0], T.sb[:, :, 8], ALU.is_lt)
    tt(["sf", "ob", "diag"], ["sx"], T.sx[:], T.sf[:].indirect(T.ob[:]), T.diag[:], ALU.mult, "gather")
    mm(["E8", "sx"], ["pA"], T.pA[0:8, 0:C], T.E8[:], T.sx[:], True, True)
    act(["pA"], ["so"], T.so[0:8, :], T.pA[0:8, 0:C], ACT.Identity, -1.0, 2.0)
    dma("S", "osg", ["so"], [], T.ys[:], T.so[0:8, :])
    emit()
